import numpy as np
import ml_dtypes


def mxq(x, axis, fmt="e4m3"):
    dtype, down = {"e4m3": (ml_dtypes.float8_e4m3fn, 7), "e5m2": (ml_dtypes.float8_e5m2, 14)}[fmt]
    v = np.moveaxis(np.asarray(x, np.float32).astype(ml_dtypes.bfloat16).astype(np.float64), axis, -1)
    blocks = v.reshape(v.shape[:-1] + (-1, 32))
    amax = np.abs(blocks).max(-1, keepdims=True)
    byte = np.maximum(np.where(amax > 0, np.frexp(amax)[1] - 1 + 127, 0) - down, 1)
    scale = np.exp2(byte - 127.0)
    codes = (blocks / scale).astype(np.float32).astype(dtype).astype(np.float64)
    return np.moveaxis((codes * scale).reshape(v.shape), -1, axis)


WIDE = False


def mx_kscale(k):
    if not WIDE:
        return np.ones(k)
    levels = np.array([10, -10, 5, -5, 0])
    if k % 512:
        return np.exp2(np.random.permutation(np.resize(levels, k // 32))).repeat(32)
    a = np.empty((k // 512, 16))
    for p in range(k // 512):
        a[p, :8] = np.random.permutation(np.resize(levels, 8))
        for g in range(8):
            far = levels[np.abs(levels - a[p, g]) >= 10]
            a[p, g + 8] = far[np.random.randint(len(far))]
    return np.exp2(a.ravel()).repeat(32)


def f64(x):
    return np.asarray(x).astype(np.float64)


def striped(idx):
    return np.tile(idx.reshape(-1, 16).T, (8, 1)).astype(np.uint16)


def unstriped(offs):
    return offs[:16].T.reshape(-1).astype(np.int64)


def gelu(v):
    return 0.5 * v * (1.0 + np.tanh(np.sqrt(2.0 / np.pi) * (v + 0.044715 * v**3)))


K, T, S, V, H, N = 1024, 2048, 512, 256, 512, 256


def setup_inputs():
    n = np.random.standard_normal
    s = mx_kscale(K)[:, None]
    u = mx_kscale(H)
    return {
        "xT": (n((K, T)) * s).astype(np.float32),
        "w1": (n((K, H)) / np.sqrt(K) / s * u).astype(np.float32),
        "w2": (n((H, N)) / np.sqrt(2 * H) / u[:, None]).astype(np.float32),
        "w3": (n((H, N)) / np.sqrt(2 * H) / u[:, None]).astype(np.float32),
        "offs": striped(np.random.permutation(T)[:S]),
    }


def reference(xT, w1, w2, w3, offs):
    xq = mxq(f64(xT)[:, unstriped(offs)], 0, "e4m3")
    h = gelu(mxq(f64(w1), 0, "e4m3").T @ xq)
    low = 0.5 * (h[:, :V] + h[:, V:2 * V])
    high = 0.5 * (h[:, :V] - h[:, V:2 * V])
    return mxq(f64(w2), 0, "e4m3").T @ mxq(low, 0, "e4m3") + mxq(f64(w3), 0, "e4m3").T @ mxq(high, 0, "e4m3")

@@ -1,0 +1,164 @@
+from contextlib import ExitStack
+
+import concourse.mybir as mybir
+
+K, T, S, V, H, N = 1024, 2048, 512, 256, 512, 256
+FLOPS = 2 * K * H * S + 2 * 2 * H * N * V
+
+F32 = mybir.dt.float32
+BF16 = mybir.dt.bfloat16
+U32 = mybir.dt.uint32
+U16 = mybir.dt.uint16
+U8 = mybir.dt.uint8
+FP8X4 = mybir.dt.float8_e4m3fn_x4
+ACT = mybir.ActivationFunctionType
+ALU = mybir.AluOpType
+
+P = 128
+PACK = 4
+K_PASS = P * PACK
+PASSES = K // K_PASS
+SLICES = 2
+PAIRS = V // SLICES
+COLS = 2 * PAIRS
+W1_SPLIT_WHOLE = 84
+W1_SPLIT_HALF = (64, 88)
+
+
+def tile_picked_haar_gelu_e_kernel(tc, xT, w1, w2, w3, offs, out):
+    nc = tc.nc
+    with ExitStack() as ctx:
+        keep = ctx.enter_context(tc.tile_pool(name="keep", bufs=1))
+        psum = ctx.enter_context(tc.psum_pool(name="psum", bufs=1))
+
+        def quantize(name, grouped, width, tag=""):
+            codes = keep.tile([P, width], U32, name=name + "_codes", align_bytes=64)
+            scales = keep.tile([P, width], U8, name=name + "_scales", align_bytes=64)
+            nc.vector.quantize_mx(out=codes[:].bitcast(FP8X4), scales=scales[:], in_=grouped)
+            return codes, scales
+
+        warm = keep.tile([P, 2], F32, name="warm")
+        nc.vector.memset(warm[:, 0:1], 0.0)
+        nc.scalar.activation(warm[:, 1:2], warm[:, 0:1], ACT.Gelu_apprx_tanh)
+
+        offsets = keep.tile([P, S // 16], U16, name="offsets")
+        x_rows = xT.rearrange("(g p t) c -> g t p c", p=P, t=PACK)
+        planes = {}
+        for g in range(PASSES):
+            for t in range(PACK):
+                planes[g, t] = keep.tile([P, T], F32, name=f"x{g}{t}")
+                nc.sync.dma_start(planes[g, t][:], x_rows[g, t])
+                if (g, t) == (0, 0):
+                    nc.sync.dma_start(offsets[:], offs)
+        w1_rows = w1.rearrange("(g p j) c -> g p j c", p=P, j=PACK)
+        w1_first = keep.tile([P, PACK, H], F32, name="w1_first")
+        nc.sync.dma_start(w1_first[:], w1_rows[0])
+        w1_halves = []
+        for u in range(2):
+            half = keep.tile([P, 2, H], F32, name=f"w1_half{u}")
+            nc.sync.dma_start(half[:], w1_rows[1, :, 2 * u : 2 * u + 2, :])
+            w1_halves.append(half)
+        w2_raw = keep.tile([P, PACK, N], F32, name="w2_raw")
+        nc.sync.dma_start(w2_raw[:], w2.rearrange("(p j) n -> p j n", j=PACK))
+        w3_raw = keep.tile([P, PACK, N], F32, name="w3_raw")
+        nc.sync.dma_start(w3_raw[:], w3.rearrange("(p j) n -> p j n", j=PACK))
+
+        xq = []
+        for g in range(PASSES):
+            picked = keep.tile([P, S, PACK], BF16, name=f"picked{g}", align_bytes=64)
+            dst = picked[:].rearrange("p (s d v) t -> p d s v t", s=SLICES, d=2)
+            for t in range(PACK):
+                nc.vector.tensor_copy(dst[:, :, :, :, t], planes[g, t][:].indirect(offsets[:]))
+            xq.append(quantize(f"x{g}", picked[:].rearrange("p c t -> p (c t)"), S))
+
+        def weave_w1(grouped, raw, j0, split):
+            rows = raw.shape[1]
+            dst = grouped[:].rearrange("p t m j -> p m j t")[:, :, j0 : j0 + rows, :]
+            src = raw[:].rearrange("p j (m t) -> p m j t", t=PACK)
+            nc.vector.tensor_copy(dst[:, :split], src[:, :split])
+            nc.scalar.copy(dst[:, split:], src[:, split:])
+
+        banks = {(s, t): psum.tile([P, COLS], F32, name=f"bank{s}{t}", tag=f"bank{s}{t}") for s in range(SLICES) for t in range(PACK)}
+
+        def layer1(g, s, t, w_codes, w_scales):
+            cols = slice(s * COLS, (s + 1) * COLS)
+            nc.tensor.matmul_mx(
+                out=banks[s, t][:],
+                lhsT=w_codes.bitcast(FP8X4),
+                lhsT_scale=w_scales,
+                rhs=xq[g][0][:, cols].bitcast(FP8X4),
+                rhs_scale=xq[g][1][:, cols],
+                start=(g == 0),
+                stop=(g == PASSES - 1),
+            )
+
+        grouped0 = keep.tile([P, PACK, P, PACK], BF16, name="w1_grouped0", align_bytes=64)
+        weave_w1(grouped0, w1_first, 0, W1_SPLIT_WHOLE)
+        w1q0 = [quantize(f"w1_0{t}", grouped0[:, t].rearrange("p m j -> p (m j)"), P) for t in range(PACK)]
+
+        grouped1 = keep.tile([P, PACK, P, PACK], BF16, name="w1_grouped1", align_bytes=64)
+        for u in range(2):
+            weave_w1(grouped1, w1_halves[u], 2 * u, W1_SPLIT_HALF[u])
+        codes1 = keep.tile([P, H], U32, name="w1_1_codes", tag="late", align_bytes=64)
+        scales1 = keep.tile([P, H], U8, name="w1_1_scales", align_bytes=64)
+        for t in range(PACK):
+            cols = slice(t * P, (t + 1) * P)
+            nc.vector.quantize_mx(
+                out=codes1[:, cols].bitcast(FP8X4),
+                scales=scales1[:, cols],
+                in_=grouped1[:, t].rearrange("p m j -> p (m j)"),
+            )
+        hidden = []
+        for s in range(SLICES):
+            h = keep.tile([P, PACK, 2, PAIRS], F32, name=f"h{s}")
+            hidden.append(h)
+            for t in range(PACK):
+                layer1(0, s, t, w1q0[t][0][:], w1q0[t][1][:])
+            for t in range(PACK):
+                cols = slice(t * P, (t + 1) * P)
+                layer1(1, s, t, codes1[:, cols], scales1[:, cols])
+                nc.scalar.activation(h[:, t].rearrange("p d v -> p (d v)"), banks[s, t][:], ACT.Gelu_apprx_tanh)
+
+        def weave(copy, grouped, raw):
+            copy(grouped[:].rearrange("p (c i) j -> p c j i", i=4), raw[:].rearrange("p j (c i) -> p c j i", i=4))
+
+        w2_grouped = keep.tile([P, N, PACK], BF16, name="w2_grouped", align_bytes=64)
+        weave(nc.vector.tensor_copy, w2_grouped, w2_raw)
+        w2q = quantize("w2", w2_grouped[:].rearrange("p n j -> p (n j)"), N)
+        w3_grouped = keep.tile([P, N, PACK], BF16, name="w3_grouped", tag="late", align_bytes=64)
+        weave(nc.scalar.copy, w3_grouped, w3_raw)
+
+        bands = []
+        for s in range(SLICES):
+            first, second = (hidden[s][:, :, d, :].rearrange("p t (c i) -> p c t i", i=4) for d in range(2))
+            grouped = []
+            for name, op in (("low", ALU.add), ("high", ALU.subtract)):
+                band = keep.tile([P, PAIRS, PACK], BF16, name=f"{name}{s}", align_bytes=64)
+                nc.vector.tensor_tensor(band[:].rearrange("p (c i) t -> p c t i", i=4), first, second, op)
+                grouped.append(band)
+            bands.append([quantize(f"band{s}{b}", band[:].rearrange("p v t -> p (v t)"), PAIRS) for b, band in enumerate(grouped)])
+            if s == 0:
+                w3q = quantize("w3", w3_grouped[:].rearrange("p n j -> p (n j)"), N)
+
+        for s in range(SLICES):
+            acc = [psum.tile([P, PAIRS], F32, name=f"acc{s}{a}", tag=f"bank0{2 * s + a}") for a in range(N // P)]
+            for b, (w_codes, w_scales) in enumerate((w2q, w3q)):
+                for a in range(N // P):
+                    cols = slice(a * P, (a + 1) * P)
+                    nc.tensor.matmul_mx(
+                        out=acc[a][:],
+                        lhsT=w_codes[:, cols].bitcast(FP8X4),
+                        lhsT_scale=w_scales[:, cols],
+                        rhs=bands[s][b][0][:].bitcast(FP8X4),
+                        rhs_scale=bands[s][b][1][:],
+                        start=(b == 0),
+                        stop=(b == 1),
+                    )
+            for a in range(N // P):
+                result = keep.tile([P, PAIRS], F32, name=f"result{s}{a}")
+                if s == SLICES - 1 and a == 1:
+                    nc.vector.tensor_scalar(result[:], acc[a][:], 0.5, None, ALU.mult)
+                    nc.sync.dma_start(out[a * P : (a + 1) * P, s * PAIRS : (s + 1) * PAIRS], result[:])
+                else:
+                    nc.scalar.activation(result[:], acc[a][:], ACT.Copy, scale=0.5)
+                    (nc.scalar if s == SLICES - 1 else nc.sync).dma_start(out[a * P : (a + 1) * P, s * PAIRS : (s + 1) * PAIRS], result[:])

@@ -21,8 +21,6 @@ PASSES = K // K_PASS
 SLICES = 2
 PAIRS = V // SLICES
 COLS = 2 * PAIRS
-W1_SPLIT_WHOLE = 84
-W1_SPLIT_HALF = (64, 88)
 
 
 def tile_picked_haar_gelu_e_kernel(tc, xT, w1, w2, w3, offs, out):
@@ -31,8 +29,8 @@ def tile_picked_haar_gelu_e_kernel(tc, xT, w1, w2, w3, offs, out):
         keep = ctx.enter_context(tc.tile_pool(name="keep", bufs=1))
         psum = ctx.enter_context(tc.psum_pool(name="psum", bufs=1))
 
-        def quantize(name, grouped, width, tag=""):
-            codes = keep.tile([P, width], U32, name=name + "_codes", align_bytes=64)
+        def quantize(name, grouped, width, tag=None):
+            codes = keep.tile([P, width], U32, name=name + "_codes", tag=tag or name + "_codes", align_bytes=64)
             scales = keep.tile([P, width], U8, name=name + "_scales", align_bytes=64)
             nc.vector.quantize_mx(out=codes[:].bitcast(FP8X4), scales=scales[:], in_=grouped)
             return codes, scales
@@ -43,6 +41,8 @@ def tile_picked_haar_gelu_e_kernel(tc, xT, w1, w2, w3, offs, out):
 
         offsets = keep.tile([P, S // 16], U16, name="offsets")
         x_rows = xT.rearrange("(g p t) c -> g t p c", p=P, t=PACK)
+        w1_rows = w1.rearrange("(g p j) c -> g p j c", p=P, j=PACK)
+        w1_first = keep.tile([P, PACK, H], F32, name="w1_first")
         planes = {}
         for g in range(PASSES):
             for t in range(PACK):
@@ -50,9 +50,8 @@ def tile_picked_haar_gelu_e_kernel(tc, xT, w1, w2, w3, offs, out):
                 nc.sync.dma_start(planes[g, t][:], x_rows[g, t])
                 if (g, t) == (0, 0):
                     nc.sync.dma_start(offsets[:], offs)
-        w1_rows = w1.rearrange("(g p j) c -> g p j c", p=P, j=PACK)
-        w1_first = keep.tile([P, PACK, H], F32, name="w1_first")
-        nc.sync.dma_start(w1_first[:], w1_rows[0])
+                if (g, t) == (1, 3):
+                    nc.sync.dma_start(w1_first[:], w1_rows[0])
         w1_halves = []
         for u in range(2):
             half = keep.tile([P, 2, H], F32, name=f"w1_half{u}")
@@ -69,44 +68,43 @@ def tile_picked_haar_gelu_e_kernel(tc, xT, w1, w2, w3, offs, out):
             dst = picked[:].rearrange("p (s d v) t -> p d s v t", s=SLICES, d=2)
             for t in range(PACK):
                 nc.vector.tensor_copy(dst[:, :, :, :, t], planes[g, t][:].indirect(offsets[:]))
-            xq.append(quantize(f"x{g}", picked[:].rearrange("p c t -> p (c t)"), S))
+            xq.append([quantize(f"x{g}{s}", picked[:, s * COLS : (s + 1) * COLS, :].rearrange("p c t -> p (c t)"), COLS) for s in range(SLICES)])
 
-        def weave_w1(grouped, raw, j0, split):
+        def weave_w1(grouped, raw, j0, copies):
             rows = raw.shape[1]
-            dst = grouped[:].rearrange("p t m j -> p m j t")[:, :, j0 : j0 + rows, :]
             src = raw[:].rearrange("p j (m t) -> p m j t", t=PACK)
-            nc.vector.tensor_copy(dst[:, :split], src[:, :split])
-            nc.scalar.copy(dst[:, split:], src[:, split:])
+            for e, copy in enumerate(copies):
+                dst = grouped[e][:].rearrange("p t m j -> p m j t")[:, :, j0 : j0 + rows, :]
+                copy(dst, src[:, :, :, 2 * e : 2 * e + 2])
 
         banks = {(s, t): psum.tile([P, COLS], F32, name=f"bank{s}{t}", tag=f"bank{s}{t}") for s in range(SLICES) for t in range(PACK)}
 
         def layer1(g, s, t, w_codes, w_scales):
-            cols = slice(s * COLS, (s + 1) * COLS)
             nc.tensor.matmul_mx(
                 out=banks[s, t][:],
                 lhsT=w_codes.bitcast(FP8X4),
                 lhsT_scale=w_scales,
-                rhs=xq[g][0][:, cols].bitcast(FP8X4),
-                rhs_scale=xq[g][1][:, cols],
+                rhs=xq[g][s][0][:].bitcast(FP8X4),
+                rhs_scale=xq[g][s][1][:],
                 start=(g == 0),
                 stop=(g == PASSES - 1),
             )
 
-        grouped0 = keep.tile([P, PACK, P, PACK], BF16, name="w1_grouped0", align_bytes=64)
-        weave_w1(grouped0, w1_first, 0, W1_SPLIT_WHOLE)
-        w1q0 = [quantize(f"w1_0{t}", grouped0[:, t].rearrange("p m j -> p (m j)"), P) for t in range(PACK)]
+        grouped0 = [keep.tile([P, 2, P, PACK], BF16, name=f"w1_grouped0{e}", tag=f"w1_grouped0{e}", align_bytes=64) for e in range(2)]
+        weave_w1(grouped0, w1_first, 0, (nc.vector.tensor_copy, nc.scalar.copy))
+        w1q0 = [quantize(f"w1_0{t}", grouped0[t // 2][:, t % 2].rearrange("p m j -> p (m j)"), P) for t in range(PACK)]
 
-        grouped1 = keep.tile([P, PACK, P, PACK], BF16, name="w1_grouped1", align_bytes=64)
-        for u in range(2):
-            weave_w1(grouped1, w1_halves[u], 2 * u, W1_SPLIT_HALF[u])
+        grouped1 = [keep.tile([P, 2, P, PACK], BF16, name=f"w1_grouped1{e}", tag=f"w1_grouped1{e}", align_bytes=64) for e in range(2)]
+        weave_w1(grouped1, w1_halves[0], 0, (nc.vector.tensor_copy, nc.scalar.copy))
+        weave_w1(grouped1, w1_halves[1], 2, (nc.vector.tensor_copy, nc.scalar.copy))
         codes1 = keep.tile([P, H], U32, name="w1_1_codes", tag="late", align_bytes=64)
-        scales1 = keep.tile([P, H], U8, name="w1_1_scales", align_bytes=64)
+        scales1 = keep.tile([P, H], U8, name="w1_1_scales", tag="late_scales", align_bytes=64)
         for t in range(PACK):
             cols = slice(t * P, (t + 1) * P)
             nc.vector.quantize_mx(
                 out=codes1[:, cols].bitcast(FP8X4),
                 scales=scales1[:, cols],
-                in_=grouped1[:, t].rearrange("p m j -> p (m j)"),
+                in_=grouped1[t // 2][:, t % 2].rearrange("p m j -> p (m j)"),
             )
         hidden = []
         for s in range(SLICES):
@@ -120,35 +118,46 @@ def tile_picked_haar_gelu_e_kernel(tc, xT, w1, w2, w3, offs, out):
                 nc.scalar.activation(h[:, t].rearrange("p d v -> p (d v)"), banks[s, t][:], ACT.Gelu_apprx_tanh)
 
         def weave(copy, grouped, raw):
-            copy(grouped[:].rearrange("p (c i) j -> p c j i", i=4), raw[:].rearrange("p j (c i) -> p c j i", i=4))
+            copy(grouped[:].rearrange("p (c i) j -> p c j i", i=4), raw.rearrange("p j (c i) -> p c j i", i=4))
 
-        w2_grouped = keep.tile([P, N, PACK], BF16, name="w2_grouped", align_bytes=64)
-        weave(nc.vector.tensor_copy, w2_grouped, w2_raw)
+        w2_grouped = keep.tile([P, N, PACK], BF16, name="w2_grouped", tag="w1_grouped11", align_bytes=64)
+        weave(nc.vector.tensor_copy, w2_grouped, w2_raw[:])
         w2q = quantize("w2", w2_grouped[:].rearrange("p n j -> p (n j)"), N)
-        w3_grouped = keep.tile([P, N, PACK], BF16, name="w3_grouped", tag="late", align_bytes=64)
-        weave(nc.scalar.copy, w3_grouped, w3_raw)
+        w3_grouped = []
+        for a in range(N // P):
+            half = keep.tile([P, P, PACK], BF16, name=f"w3_grouped{a}", tag=("late", "late_scales")[a], align_bytes=64)
+            weave(nc.scalar.copy, half, w3_raw[:, :, a * P : (a + 1) * P])
+            w3_grouped.append(half)
 
-        bands = []
-        for s in range(SLICES):
+        def band(name, s, op, tag):
             first, second = (hidden[s][:, :, d, :].rearrange("p t (c i) -> p c t i", i=4) for d in range(2))
-            grouped = []
-            for name, op in (("low", ALU.add), ("high", ALU.subtract)):
-                band = keep.tile([P, PAIRS, PACK], BF16, name=f"{name}{s}", align_bytes=64)
-                nc.vector.tensor_tensor(band[:].rearrange("p (c i) t -> p c t i", i=4), first, second, op)
-                grouped.append(band)
-            bands.append([quantize(f"band{s}{b}", band[:].rearrange("p v t -> p (v t)"), PAIRS) for b, band in enumerate(grouped)])
-            if s == 0:
-                w3q = quantize("w3", w3_grouped[:].rearrange("p n j -> p (n j)"), N)
+            values = keep.tile([P, PAIRS, PACK], BF16, name=f"{name}{s}", tag=tag, align_bytes=64)
+            nc.vector.tensor_tensor(values[:].rearrange("p (c i) t -> p c t i", i=4), first, second, op)
+            return values[:].rearrange("p v t -> p (v t)")
+
+        def flat(grouped):
+            return grouped[:].rearrange("p n j -> p (n j)")
+
+        low0 = band("low", 0, ALU.add, "low0")
+        high0 = band("high", 0, ALU.subtract, "high0")
+        bands = [[quantize("low0q", low0, PAIRS), quantize("high0q", high0, PAIRS)]]
+        low1 = band("low", 1, ALU.add, "low1")
+        w3q = [quantize("w3a", flat(w3_grouped[0]), P)]
+        low1q = quantize("low1q", low1, PAIRS)
+        high1 = band("high", 1, ALU.subtract, "high1")
+        w3q.append(quantize("w3b", flat(w3_grouped[1]), P))
+        bands.append([low1q, quantize("high1q", high1, PAIRS)])
+        w2q = [(w2q[0][:, a * P : (a + 1) * P], w2q[1][:, a * P : (a + 1) * P]) for a in range(N // P)]
+        w3q = [(c[:], sc[:]) for c, sc in w3q]
 
         for s in range(SLICES):
             acc = [psum.tile([P, PAIRS], F32, name=f"acc{s}{a}", tag=f"bank0{2 * s + a}") for a in range(N // P)]
-            for b, (w_codes, w_scales) in enumerate((w2q, w3q)):
+            for b, wq in enumerate((w2q, w3q)):
                 for a in range(N // P):
-                    cols = slice(a * P, (a + 1) * P)
                     nc.tensor.matmul_mx(
                         out=acc[a][:],
-                        lhsT=w_codes[:, cols].bitcast(FP8X4),
-                        lhsT_scale=w_scales[:, cols],
+                        lhsT=wq[a][0].bitcast(FP8X4),
+                        lhsT_scale=wq[a][1],
                         rhs=bands[s][b][0][:].bitcast(FP8X4),
                         rhs_scale=bands[s][b][1][:],
                         start=(b == 0),

@@ -52,11 +52,11 @@ def tile_picked_haar_gelu_e_kernel(tc, xT, w1, w2, w3, offs, out):
                     nc.sync.dma_start(offsets[:], offs)
                 if (g, t) == (1, 3):
                     nc.sync.dma_start(w1_first[:], w1_rows[0])
-        w1_halves = []
-        for u in range(2):
-            half = keep.tile([P, 2, H], F32, name=f"w1_half{u}")
-            nc.sync.dma_start(half[:], w1_rows[1, :, 2 * u : 2 * u + 2, :])
-            w1_halves.append(half)
+        w1_pieces = []
+        for j0, m0, m1 in ((0, 0, P), (2, 0, 96), (2, 96, P)):
+            piece = keep.tile([P, 2, PACK * (m1 - m0)], F32, name=f"w1_piece{j0}{m0}")
+            nc.sync.dma_start(piece[:], w1_rows[1, :, j0 : j0 + 2, PACK * m0 : PACK * m1])
+            w1_pieces.append((piece, j0, m0))
         w2_raw = keep.tile([P, PACK, N], F32, name="w2_raw")
         nc.sync.dma_start(w2_raw[:], w2.rearrange("(p j) n -> p j n", j=PACK))
         w3_raw = keep.tile([P, PACK, N], F32, name="w3_raw")
@@ -70,11 +70,11 @@ def tile_picked_haar_gelu_e_kernel(tc, xT, w1, w2, w3, offs, out):
                 nc.vector.tensor_copy(dst[:, :, :, :, t], planes[g, t][:].indirect(offsets[:]))
             xq.append([quantize(f"x{g}{s}", picked[:, s * COLS : (s + 1) * COLS, :].rearrange("p c t -> p (c t)"), COLS) for s in range(SLICES)])
 
-        def weave_w1(grouped, raw, j0, copies):
+        def weave_w1(grouped, raw, j0, m0):
             rows = raw.shape[1]
             src = raw[:].rearrange("p j (m t) -> p m j t", t=PACK)
-            for e, copy in enumerate(copies):
-                dst = grouped[e][:].rearrange("p t m j -> p m j t")[:, :, j0 : j0 + rows, :]
+            for e, copy in enumerate((nc.vector.tensor_copy, nc.scalar.copy)):
+                dst = grouped[e][:].rearrange("p t m j -> p m j t")[:, m0 : m0 + raw.shape[2] // PACK, j0 : j0 + rows, :]
                 copy(dst, src[:, :, :, 2 * e : 2 * e + 2])
 
         banks = {(s, t): psum.tile([P, COLS], F32, name=f"bank{s}{t}", tag=f"bank{s}{t}") for s in range(SLICES) for t in range(PACK)}
@@ -90,13 +90,23 @@ def tile_picked_haar_gelu_e_kernel(tc, xT, w1, w2, w3, offs, out):
                 stop=(g == PASSES - 1),
             )
 
+        for i in range(4):
+            nc.tensor.matmul_mx(
+                out=banks[SLICES - 1, PACK - 1][:],
+                lhsT=xq[1][0][0][:, :P].bitcast(FP8X4),
+                lhsT_scale=xq[1][0][1][:, :P],
+                rhs=xq[1][0][0][:].bitcast(FP8X4),
+                rhs_scale=xq[1][0][1][:],
+                start=True,
+                stop=True,
+            )
         grouped0 = [keep.tile([P, 2, P, PACK], BF16, name=f"w1_grouped0{e}", tag=f"w1_grouped0{e}", align_bytes=64) for e in range(2)]
-        weave_w1(grouped0, w1_first, 0, (nc.vector.tensor_copy, nc.scalar.copy))
+        weave_w1(grouped0, w1_first, 0, 0)
         w1q0 = [quantize(f"w1_0{t}", grouped0[t // 2][:, t % 2].rearrange("p m j -> p (m j)"), P) for t in range(PACK)]
 
         grouped1 = [keep.tile([P, 2, P, PACK], BF16, name=f"w1_grouped1{e}", tag=f"w1_grouped1{e}", align_bytes=64) for e in range(2)]
-        weave_w1(grouped1, w1_halves[0], 0, (nc.vector.tensor_copy, nc.scalar.copy))
-        weave_w1(grouped1, w1_halves[1], 2, (nc.vector.tensor_copy, nc.scalar.copy))
+        for piece, j0, m0 in w1_pieces:
+            weave_w1(grouped1, piece, j0, m0)
         codes1 = keep.tile([P, H], U32, name="w1_1_codes", tag="late", align_bytes=64)
         scales1 = keep.tile([P, H], U8, name="w1_1_scales", tag="late_scales", align_bytes=64)
         for t in range(PACK):

@@ -21,6 +21,7 @@ PASSES = K // K_PASS
 SLICES = 2
 PAIRS = V // SLICES
 COLS = 2 * PAIRS
+HALF = P // 2
 
 
 def tile_picked_haar_gelu_e_kernel(tc, xT, w1, w2, w3, offs, out):
@@ -29,11 +30,27 @@ def tile_picked_haar_gelu_e_kernel(tc, xT, w1, w2, w3, offs, out):
         keep = ctx.enter_context(tc.tile_pool(name="keep", bufs=1))
         psum = ctx.enter_context(tc.psum_pool(name="psum", bufs=1))
 
-        def quantize(name, grouped, width, tag=None):
-            codes = keep.tile([P, width], U32, name=name + "_codes", tag=tag or name + "_codes", align_bytes=64)
+        def mx_tiles(name, width):
+            codes = keep.tile([P, width], U32, name=name + "_codes", align_bytes=64)
             scales = keep.tile([P, width], U8, name=name + "_scales", align_bytes=64)
-            nc.vector.quantize_mx(out=codes[:].bitcast(FP8X4), scales=scales[:], in_=grouped)
             return codes, scales
+
+        def quantize(mx, cols, grouped):
+            nc.vector.quantize_mx(out=mx[0][:, cols].bitcast(FP8X4), scales=mx[1][:, cols], in_=grouped)
+
+        def matmul(acc, w_mx, w_cols, x_mx, x_cols, start, stop):
+            nc.tensor.matmul_mx(
+                out=acc,
+                lhsT=w_mx[0][:, w_cols].bitcast(FP8X4),
+                lhsT_scale=w_mx[1][:, w_cols],
+                rhs=x_mx[0][:, x_cols].bitcast(FP8X4),
+                rhs_scale=x_mx[1][:, x_cols],
+                start=start,
+                stop=stop,
+            )
+
+        def span(i, width):
+            return slice(i * width, (i + 1) * width)
 
         warm = keep.tile([P, 2], F32, name="warm")
         nc.vector.memset(warm[:, 0:1], 0.0)
@@ -42,23 +59,27 @@ def tile_picked_haar_gelu_e_kernel(tc, xT, w1, w2, w3, offs, out):
         offsets = keep.tile([P, S // 16], U16, name="offsets")
         x_rows = xT.rearrange("(g p t) c -> g t p c", p=P, t=PACK)
         w1_rows = w1.rearrange("(g p j) c -> g p j c", p=P, j=PACK)
-        w1_first = keep.tile([P, PACK, H], F32, name="w1_first")
+
+        def load_w1(g, m0, m1):
+            piece = keep.tile([P, PACK, PACK * (m1 - m0)], F32, name=f"w1_piece{g}_{m0}")
+            nc.sync.dma_start(piece[:], w1_rows[g, :, :, PACK * m0 : PACK * m1])
+            return piece
+
         planes = {}
         for g in range(PASSES):
             for t in range(PACK):
+                if (g, t) == (PASSES - 1, PACK - 1):
+                    w1_first = load_w1(0, 0, P)
                 planes[g, t] = keep.tile([P, T], F32, name=f"x{g}{t}")
                 nc.sync.dma_start(planes[g, t][:], x_rows[g, t])
                 if (g, t) == (0, 0):
                     nc.sync.dma_start(offsets[:], offs)
-                if (g, t) == (1, 3):
-                    nc.sync.dma_start(w1_first[:], w1_rows[0])
-        w1_pieces = []
-        for j0, m0, m1 in ((0, 0, P), (2, 0, 96), (2, 96, P)):
-            piece = keep.tile([P, 2, PACK * (m1 - m0)], F32, name=f"w1_piece{j0}{m0}")
-            nc.sync.dma_start(piece[:], w1_rows[1, :, j0 : j0 + 2, PACK * m0 : PACK * m1])
-            w1_pieces.append((piece, j0, m0))
-        w2_raw = keep.tile([P, PACK, N], F32, name="w2_raw")
-        nc.sync.dma_start(w2_raw[:], w2.rearrange("(p j) n -> p j n", j=PACK))
+        w1_last = [load_w1(1, m0, m1) for m0, m1 in ((0, HALF), (HALF, 96), (96, P))]
+        w2_raw = []
+        for a in range(N // P):
+            half = keep.tile([P, PACK, P], F32, name=f"w2_raw{a}")
+            nc.sync.dma_start(half[:], w2.rearrange("(p j) n -> p j n", j=PACK)[:, :, span(a, P)])
+            w2_raw.append(half)
         w3_raw = keep.tile([P, PACK, N], F32, name="w3_raw")
         nc.sync.dma_start(w3_raw[:], w3.rearrange("(p j) n -> p j n", j=PACK))
 
@@ -68,116 +89,119 @@ def tile_picked_haar_gelu_e_kernel(tc, xT, w1, w2, w3, offs, out):
             dst = picked[:].rearrange("p (s d v) t -> p d s v t", s=SLICES, d=2)
             for t in range(PACK):
                 nc.vector.tensor_copy(dst[:, :, :, :, t], planes[g, t][:].indirect(offsets[:]))
-            xq.append([quantize(f"x{g}{s}", picked[:, s * COLS : (s + 1) * COLS, :].rearrange("p c t -> p (c t)"), COLS) for s in range(SLICES)])
+            xq.append(mx_tiles(f"xq{g}", S if g == 0 else COLS))
+            quantize(xq[g], slice(0, S if g == 0 else COLS), picked[:, : S if g == 0 else COLS].rearrange("p c t -> p (c t)"))
 
-        def weave_w1(grouped, raw, j0, m0):
-            rows = raw.shape[1]
-            src = raw[:].rearrange("p j (m t) -> p m j t", t=PACK)
-            for e, copy in enumerate((nc.vector.tensor_copy, nc.scalar.copy)):
-                dst = grouped[e][:].rearrange("p t m j -> p m j t")[:, m0 : m0 + raw.shape[2] // PACK, j0 : j0 + rows, :]
-                copy(dst, src[:, :, :, 2 * e : 2 * e + 2])
+        def weave_w1(copy, grouped, raw, e):
+            src = raw.rearrange("p j (m t) -> p m j t", t=PACK)[:, :, :, 2 * e : 2 * e + 2]
+            copy(grouped.rearrange("p t m j -> p m j t"), src)
 
-        banks = {(s, t): psum.tile([P, COLS], F32, name=f"bank{s}{t}", tag=f"bank{s}{t}") for s in range(SLICES) for t in range(PACK)}
-
-        def layer1(g, s, t, w_codes, w_scales):
-            nc.tensor.matmul_mx(
-                out=banks[s, t][:],
-                lhsT=w_codes.bitcast(FP8X4),
-                lhsT_scale=w_scales,
-                rhs=xq[g][s][0][:].bitcast(FP8X4),
-                rhs_scale=xq[g][s][1][:],
-                start=(g == 0),
-                stop=(g == PASSES - 1),
-            )
-
-        for i in range(4):
-            nc.tensor.matmul_mx(
-                out=banks[SLICES - 1, PACK - 1][:],
-                lhsT=xq[1][0][0][:, :P].bitcast(FP8X4),
-                lhsT_scale=xq[1][0][1][:, :P],
-                rhs=xq[1][0][0][:].bitcast(FP8X4),
-                rhs_scale=xq[1][0][1][:],
-                start=True,
-                stop=True,
-            )
-        grouped0 = [keep.tile([P, 2, P, PACK], BF16, name=f"w1_grouped0{e}", tag=f"w1_grouped0{e}", align_bytes=64) for e in range(2)]
-        weave_w1(grouped0, w1_first, 0, 0)
-        w1q0 = [quantize(f"w1_0{t}", grouped0[t // 2][:, t % 2].rearrange("p m j -> p (m j)"), P) for t in range(PACK)]
-
-        grouped1 = [keep.tile([P, 2, P, PACK], BF16, name=f"w1_grouped1{e}", tag=f"w1_grouped1{e}", align_bytes=64) for e in range(2)]
-        for piece, j0, m0 in w1_pieces:
-            weave_w1(grouped1, piece, j0, m0)
-        codes1 = keep.tile([P, H], U32, name="w1_1_codes", tag="late", align_bytes=64)
-        scales1 = keep.tile([P, H], U8, name="w1_1_scales", tag="late_scales", align_bytes=64)
+        engines = (nc.vector.tensor_copy, nc.scalar.copy)
+        grouped0 = [keep.tile([P, 2, P, PACK], BF16, name=f"w1_grouped0{e}", align_bytes=64) for e in range(2)]
+        for e in range(2):
+            weave_w1(engines[e], grouped0[e][:], w1_first[:], e)
+        w1q = [[mx_tiles(f"w1q{g}{t}", P) for t in range(PACK)] for g in range(PASSES)]
         for t in range(PACK):
-            cols = slice(t * P, (t + 1) * P)
-            nc.vector.quantize_mx(
-                out=codes1[:, cols].bitcast(FP8X4),
-                scales=scales1[:, cols],
-                in_=grouped1[t // 2][:, t % 2].rearrange("p m j -> p (m j)"),
-            )
-        hidden = []
-        for s in range(SLICES):
-            h = keep.tile([P, PACK, 2, PAIRS], F32, name=f"h{s}")
-            hidden.append(h)
-            for t in range(PACK):
-                layer1(0, s, t, w1q0[t][0][:], w1q0[t][1][:])
-            for t in range(PACK):
-                cols = slice(t * P, (t + 1) * P)
-                layer1(1, s, t, codes1[:, cols], scales1[:, cols])
-                nc.scalar.activation(h[:, t].rearrange("p d v -> p (d v)"), banks[s, t][:], ACT.Gelu_apprx_tanh)
+            quantize(w1q[0][t], slice(0, P), grouped0[t // 2][:, t % 2].rearrange("p m j -> p (m j)"))
+
+        grouped1 = {(u, e): keep.tile([P, 2, HALF, PACK], BF16, name=f"w1_grouped1{u}{e}", tag=f"w1_grouped1{u}{e}", align_bytes=64) for u in range(2) for e in range(2)}
+        for e in range(2):
+            weave_w1(nc.scalar.copy, grouped1[0, e][:], w1_last[0][:], e)
+        for q in range(2):
+            for e in range(2):
+                weave_w1(engines[e], grouped1[1, e][:, :, span(q, 32), :], w1_last[1 + q][:], e)
+        for t in range(PACK):
+            for u in range(2):
+                quantize(w1q[1][t], span(u, HALF), grouped1[u, t // 2][:, t % 2].rearrange("p m j -> p (m j)"))
+        late_codes = keep.tile([P, COLS], U32, name="late_codes", tag="w1_grouped110", align_bytes=64)
+        late_scales = keep.tile([P, COLS], U8, name="late_scales", align_bytes=64)
+        quantize((late_codes, late_scales), slice(0, COLS), picked[:, COLS:].rearrange("p c t -> p (c t)"))
+        x_mx = {(0, 0): (xq[0], span(0, COLS)), (0, 1): (xq[0], span(1, COLS)), (1, 0): (xq[1], span(0, COLS)), (1, 1): ((late_codes, late_scales), span(0, COLS))}
 
         def weave(copy, grouped, raw):
-            copy(grouped[:].rearrange("p (c i) j -> p c j i", i=4), raw.rearrange("p j (c i) -> p c j i", i=4))
+            copy(grouped.rearrange("p (c i) j -> p c j i", i=4), raw.rearrange("p j (c i) -> p c j i", i=4))
 
-        w2_grouped = keep.tile([P, N, PACK], BF16, name="w2_grouped", tag="w1_grouped11", align_bytes=64)
-        weave(nc.vector.tensor_copy, w2_grouped, w2_raw[:])
-        w2q = quantize("w2", w2_grouped[:].rearrange("p n j -> p (n j)"), N)
-        w3_grouped = []
-        for a in range(N // P):
-            half = keep.tile([P, P, PACK], BF16, name=f"w3_grouped{a}", tag=("late", "late_scales")[a], align_bytes=64)
-            weave(nc.scalar.copy, half, w3_raw[:, :, a * P : (a + 1) * P])
-            w3_grouped.append(half)
+        w2_grouped = [keep.tile([P, P, PACK], BF16, name=f"w2_grouped{a}", align_bytes=64) for a in range(N // P)]
+        weave(nc.scalar.copy, w2_grouped[0][:], w2_raw[0][:])
+        weave(nc.vector.tensor_copy, w2_grouped[1][:], w2_raw[1][:])
 
-        def band(name, s, op, tag):
-            first, second = (hidden[s][:, :, d, :].rearrange("p t (c i) -> p c t i", i=4) for d in range(2))
-            values = keep.tile([P, PAIRS, PACK], BF16, name=f"{name}{s}", tag=tag, align_bytes=64)
-            nc.vector.tensor_tensor(values[:].rearrange("p (c i) t -> p c t i", i=4), first, second, op)
-            return values[:].rearrange("p v t -> p (v t)")
+        banks = {(s, t): psum.tile([P, 2, PAIRS], F32, name=f"bank{s}{t}", tag=f"bank{s}{t}") for s in range(SLICES) for t in range(PACK)}
+        for s in range(SLICES):
+            for g in range(PASSES):
+                for t in range(PACK):
+                    matmul(banks[s, t][:].rearrange("p d v -> p (d v)"), w1q[g][t], slice(0, P), *x_mx[g, s], g == 0, g == PASSES - 1)
+
+        def gelu(name, s, v0, v1):
+            h = keep.tile([P, PACK, 2, v1 - v0], F32, name=name)
+            for t in range(PACK):
+                nc.scalar.activation(h[:, t], banks[s, t][:, :, v0:v1], ACT.Gelu_apprx_tanh)
+            return h
+
+        h0 = [gelu(f"h0{u}", 0, HALF * u, HALF * (u + 1)) for u in range(2)]
+        h1 = gelu("h1", 1, 0, PAIRS)
+
+        for t in range(2):
+            spare = psum.tile([P, S], F32, name=f"spare{t}", tag=f"bank1{2 + t}")
+            matmul(spare[:], w1q[1][t], slice(0, P), xq[0], slice(0, S), True, True)
 
         def flat(grouped):
-            return grouped[:].rearrange("p n j -> p (n j)")
+            return grouped.rearrange("p n j -> p (n j)")
 
-        low0 = band("low", 0, ALU.add, "low0")
-        high0 = band("high", 0, ALU.subtract, "high0")
-        bands = [[quantize("low0q", low0, PAIRS), quantize("high0q", high0, PAIRS)]]
-        low1 = band("low", 1, ALU.add, "low1")
-        w3q = [quantize("w3a", flat(w3_grouped[0]), P)]
-        low1q = quantize("low1q", low1, PAIRS)
-        high1 = band("high", 1, ALU.subtract, "high1")
-        w3q.append(quantize("w3b", flat(w3_grouped[1]), P))
-        bands.append([low1q, quantize("high1q", high1, PAIRS)])
-        w2q = [(w2q[0][:, a * P : (a + 1) * P], w2q[1][:, a * P : (a + 1) * P]) for a in range(N // P)]
-        w3q = [(c[:], sc[:]) for c, sc in w3q]
+        def band(values, h, op):
+            first, second = (h[:, :, d, :].rearrange("p t (c i) -> p c t i", i=2) for d in range(2))
+            nc.vector.tensor_tensor(values.rearrange("p (c i) t -> p c t i", i=2), first, second, op)
 
+        w3_grouped = []
+        for a in range(N // P):
+            half = keep.tile([P, P, PACK], BF16, name=f"w3_grouped{a}", align_bytes=64)
+            weave(nc.scalar.copy, half[:], w3_raw[:, :, span(a, P)])
+            w3_grouped.append(half)
+
+        w2q = mx_tiles("w2q", N)
+        w3q = [mx_tiles(f"w3q{a}", P) for a in range(N // P)]
+        bands0 = keep.tile([P, 2, PAIRS, PACK], BF16, name="bands0", align_bytes=64)
+        bands0q = mx_tiles("bands0q", 2 * PAIRS)
+        quantize(w2q, span(0, P), flat(w2_grouped[0][:]))
+        for u in range(2):
+            band(bands0[:, 0, span(u, HALF)], h0[u], ALU.add)
+            band(bands0[:, 1, span(u, HALF)], h0[u], ALU.subtract)
+            if u == 0:
+                quantize(w2q, span(1, P), flat(w2_grouped[1][:]))
+        low1 = keep.tile([P, PAIRS, PACK], BF16, name="low1", align_bytes=64)
+        high1 = keep.tile([P, PAIRS, PACK], BF16, name="high1", align_bytes=64)
+        low1q, high1q = mx_tiles("low1q", PAIRS), mx_tiles("high1q", PAIRS)
+        quantize(bands0q, slice(0, 2 * PAIRS), bands0[:].rearrange("p b v t -> p (b v t)"))
+        band(low1[:], h1, ALU.add)
+        quantize(w3q[0], slice(0, P), flat(w3_grouped[0][:]))
+        band(high1[:], h1, ALU.subtract)
+        quantize(low1q, slice(0, PAIRS), flat(low1[:]))
+        quantize(w3q[1], slice(0, P), flat(w3_grouped[1][:]))
+        quantize(high1q, slice(0, PAIRS), flat(high1[:]))
+        low = [(bands0q, span(0, PAIRS)), (low1q, span(0, PAIRS))]
+        high = [(bands0q, span(1, PAIRS)), (high1q, span(0, PAIRS))]
+
+        acc = {(s, a): psum.tile([P, PAIRS], F32, name=f"acc{s}{a}", tag=f"bank0{2 * s + a}") for s in range(SLICES) for a in range(N // P)}
+
+        def low_pass(s, a):
+            matmul(acc[s, a][:], w2q, span(a, P), *low[s], True, False)
+
+        def high_pass(s, a):
+            matmul(acc[s, a][:], w3q[a], slice(0, P), *high[s], False, True)
+
+        low_pass(0, 0)
+        low_pass(0, 1)
+        high_pass(0, 0)
+        low_pass(1, 0)
+        low_pass(1, 1)
+        high_pass(0, 1)
+        high_pass(1, 0)
+        high_pass(1, 1)
         for s in range(SLICES):
-            acc = [psum.tile([P, PAIRS], F32, name=f"acc{s}{a}", tag=f"bank0{2 * s + a}") for a in range(N // P)]
-            for b, wq in enumerate((w2q, w3q)):
-                for a in range(N // P):
-                    nc.tensor.matmul_mx(
-                        out=acc[a][:],
-                        lhsT=wq[a][0].bitcast(FP8X4),
-                        lhsT_scale=wq[a][1],
-                        rhs=bands[s][b][0][:].bitcast(FP8X4),
-                        rhs_scale=bands[s][b][1][:],
-                        start=(b == 0),
-                        stop=(b == 1),
-                    )
             for a in range(N // P):
                 result = keep.tile([P, PAIRS], F32, name=f"result{s}{a}")
                 if s == SLICES - 1 and a == 1:
-                    nc.vector.tensor_scalar(result[:], acc[a][:], 0.5, None, ALU.mult)
-                    nc.sync.dma_start(out[a * P : (a + 1) * P, s * PAIRS : (s + 1) * PAIRS], result[:])
+                    nc.vector.tensor_scalar(result[:], acc[s, a][:], 0.5, None, ALU.mult)
+                    nc.sync.dma_start(out[span(a, P), span(s, PAIRS)], result[:])
                 else:
-                    nc.scalar.activation(result[:], acc[a][:], ACT.Copy, scale=0.5)
-                    (nc.scalar if s == SLICES - 1 else nc.sync).dma_start(out[a * P : (a + 1) * P, s * PAIRS : (s + 1) * PAIRS], result[:])
+                    nc.scalar.activation(result[:], acc[s, a][:], ACT.Copy, scale=0.5)
+                    (nc.scalar if s == SLICES - 1 else nc.sync).dma_start(out[span(a, P), span(s, PAIRS)], result[:])

@@ -57,29 +57,28 @@ def tile_picked_haar_gelu_e_kernel(tc, xT, w1, w2, w3, offs, out):
         nc.scalar.activation(warm[:, 1:2], warm[:, 0:1], ACT.Gelu_apprx_tanh)
 
         offsets = keep.tile([P, S // 16], U16, name="offsets")
-        x_rows = xT.rearrange("(g p t) c -> g t p c", p=P, t=PACK)
+        x_rows = xT.rearrange("(g p t) c -> g p t c", p=P, t=PACK)
         w1_rows = w1.rearrange("(g p j) c -> g p j c", p=P, j=PACK)
 
-        def load_w1(g, m0, m1):
-            piece = keep.tile([P, PACK, PACK * (m1 - m0)], F32, name=f"w1_piece{g}_{m0}")
-            nc.sync.dma_start(piece[:], w1_rows[g, :, :, PACK * m0 : PACK * m1])
+        def load_w1(g, j0, j1, m0, m1):
+            piece = keep.tile([P, j1 - j0, PACK * (m1 - m0)], F32, name=f"w1_piece{g}_{j0}_{m0}")
+            nc.sync.dma_start(piece[:], w1_rows[g, :, j0:j1, PACK * m0 : PACK * m1])
             return piece
 
         planes = {}
-        for g in range(PASSES):
-            for t in range(PACK):
-                if (g, t) == (PASSES - 1, PACK - 1):
-                    w1_first = load_w1(0, 0, P)
-                planes[g, t] = keep.tile([P, T], F32, name=f"x{g}{t}")
-                nc.sync.dma_start(planes[g, t][:], x_rows[g, t])
-                if (g, t) == (0, 0):
+        for g, rows in enumerate((2, 1)):
+            for t0 in range(0, PACK, rows):
+                loaded = keep.tile([P, rows, T], F32, name=f"x{g}{t0}")
+                nc.sync.dma_start(loaded[:], x_rows[g, :, t0 : t0 + rows])
+                for t in range(rows):
+                    planes[g, t0 + t] = loaded[:, t]
+                if (g, t0) == (0, 0):
                     nc.sync.dma_start(offsets[:], offs)
-        w1_last = [load_w1(1, m0, m1) for m0, m1 in ((0, HALF), (HALF, 96), (96, P))]
-        w2_raw = []
-        for a in range(N // P):
-            half = keep.tile([P, PACK, P], F32, name=f"w2_raw{a}")
-            nc.sync.dma_start(half[:], w2.rearrange("(p j) n -> p j n", j=PACK)[:, :, span(a, P)])
-            w2_raw.append(half)
+        w1_first = load_w1(0, 0, PACK, 0, P)
+        pieces = ((0, 0, P), (2, 0, 96), (2, 96, P))
+        w1_last = [load_w1(1, j0, j0 + 2, m0, m1) for j0, m0, m1 in pieces]
+        w2_raw = keep.tile([P, PACK, N], F32, name="w2_raw")
+        nc.sync.dma_start(w2_raw[:], w2.rearrange("(p j) n -> p j n", j=PACK))
         w3_raw = keep.tile([P, PACK, N], F32, name="w3_raw")
         nc.sync.dma_start(w3_raw[:], w3.rearrange("(p j) n -> p j n", j=PACK))
 
@@ -88,9 +87,13 @@ def tile_picked_haar_gelu_e_kernel(tc, xT, w1, w2, w3, offs, out):
             picked = keep.tile([P, S, PACK], BF16, name=f"picked{g}", align_bytes=64)
             dst = picked[:].rearrange("p (s d v) t -> p d s v t", s=SLICES, d=2)
             for t in range(PACK):
-                nc.vector.tensor_copy(dst[:, :, :, :, t], planes[g, t][:].indirect(offsets[:]))
-            xq.append(mx_tiles(f"xq{g}", S if g == 0 else COLS))
-            quantize(xq[g], slice(0, S if g == 0 else COLS), picked[:, : S if g == 0 else COLS].rearrange("p c t -> p (c t)"))
+                nc.vector.tensor_copy(dst[:, :, :, :, t], planes[g, t].indirect(offsets[:]))
+            xq.append(mx_tiles(f"xq{g}", S))
+            quantize(xq[g], slice(0, S), picked[:].rearrange("p c t -> p (c t)"))
+
+        for t in range(2):
+            spare = psum.tile([P, S], F32, name=f"spare{t}", tag=f"bank1{2 + t}")
+            matmul(spare[:], xq[1], slice(0, P), xq[1], slice(0, S), True, True)
 
         def weave_w1(copy, grouped, raw, e):
             src = raw.rearrange("p j (m t) -> p m j t", t=PACK)[:, :, :, 2 * e : 2 * e + 2]
@@ -104,32 +107,25 @@ def tile_picked_haar_gelu_e_kernel(tc, xT, w1, w2, w3, offs, out):
         for t in range(PACK):
             quantize(w1q[0][t], slice(0, P), grouped0[t // 2][:, t % 2].rearrange("p m j -> p (m j)"))
 
-        grouped1 = {(u, e): keep.tile([P, 2, HALF, PACK], BF16, name=f"w1_grouped1{u}{e}", tag=f"w1_grouped1{u}{e}", align_bytes=64) for u in range(2) for e in range(2)}
-        for e in range(2):
-            weave_w1(nc.scalar.copy, grouped1[0, e][:], w1_last[0][:], e)
-        for q in range(2):
+        grouped1 = [keep.tile([P, 2, P, PACK], BF16, name=f"w1_grouped1{e}", tag=f"w1_grouped1{e}", align_bytes=64) for e in range(2)]
+        for raw, (j0, m0, m1) in zip(w1_last, pieces):
             for e in range(2):
-                weave_w1(engines[e], grouped1[1, e][:, :, span(q, 32), :], w1_last[1 + q][:], e)
+                weave_w1(engines[e], grouped1[e][:, :, m0:m1, j0 : j0 + 2], raw[:], e)
         for t in range(PACK):
-            for u in range(2):
-                quantize(w1q[1][t], span(u, HALF), grouped1[u, t // 2][:, t % 2].rearrange("p m j -> p (m j)"))
-        late_codes = keep.tile([P, COLS], U32, name="late_codes", tag="w1_grouped110", align_bytes=64)
-        late_scales = keep.tile([P, COLS], U8, name="late_scales", align_bytes=64)
-        quantize((late_codes, late_scales), slice(0, COLS), picked[:, COLS:].rearrange("p c t -> p (c t)"))
-        x_mx = {(0, 0): (xq[0], span(0, COLS)), (0, 1): (xq[0], span(1, COLS)), (1, 0): (xq[1], span(0, COLS)), (1, 1): ((late_codes, late_scales), span(0, COLS))}
+            quantize(w1q[1][t], slice(0, P), grouped1[t // 2][:, t % 2].rearrange("p m j -> p (m j)"))
 
         def weave(copy, grouped, raw):
             copy(grouped.rearrange("p (c i) j -> p c j i", i=4), raw.rearrange("p j (c i) -> p c j i", i=4))
 
-        w2_grouped = [keep.tile([P, P, PACK], BF16, name=f"w2_grouped{a}", align_bytes=64) for a in range(N // P)]
-        weave(nc.scalar.copy, w2_grouped[0][:], w2_raw[0][:])
-        weave(nc.vector.tensor_copy, w2_grouped[1][:], w2_raw[1][:])
+        w2_grouped = [keep.tile([P, P, PACK], BF16, name=f"w2_grouped{a}", tag=f"w1_grouped1{a}", align_bytes=64) for a in range(N // P)]
+        for a in range(N // P):
+            weave(nc.vector.tensor_copy, w2_grouped[a][:], w2_raw[:, :, span(a, P)])
 
         banks = {(s, t): psum.tile([P, 2, PAIRS], F32, name=f"bank{s}{t}", tag=f"bank{s}{t}") for s in range(SLICES) for t in range(PACK)}
         for s in range(SLICES):
             for g in range(PASSES):
                 for t in range(PACK):
-                    matmul(banks[s, t][:].rearrange("p d v -> p (d v)"), w1q[g][t], slice(0, P), *x_mx[g, s], g == 0, g == PASSES - 1)
+                    matmul(banks[s, t][:].rearrange("p d v -> p (d v)"), w1q[g][t], slice(0, P), xq[g], span(s, COLS), g == 0, g == PASSES - 1)
 
         def gelu(name, s, v0, v1):
             h = keep.tile([P, PACK, 2, v1 - v0], F32, name=name)
@@ -139,10 +135,6 @@ def tile_picked_haar_gelu_e_kernel(tc, xT, w1, w2, w3, offs, out):
 
         h0 = [gelu(f"h0{u}", 0, HALF * u, HALF * (u + 1)) for u in range(2)]
         h1 = gelu("h1", 1, 0, PAIRS)
-
-        for t in range(2):
-            spare = psum.tile([P, S], F32, name=f"spare{t}", tag=f"bank1{2 + t}")
-            matmul(spare[:], w1q[1][t], slice(0, P), xq[0], slice(0, S), True, True)
 
         def flat(grouped):
             return grouped.rearrange("p n j -> p (n j)")
@@ -158,15 +150,14 @@ def tile_picked_haar_gelu_e_kernel(tc, xT, w1, w2, w3, offs, out):
             w3_grouped.append(half)
 
         w2q = mx_tiles("w2q", N)
+        for a in range(N // P):
+            quantize(w2q, span(a, P), flat(w2_grouped[a][:]))
         w3q = [mx_tiles(f"w3q{a}", P) for a in range(N // P)]
         bands0 = keep.tile([P, 2, PAIRS, PACK], BF16, name="bands0", align_bytes=64)
         bands0q = mx_tiles("bands0q", 2 * PAIRS)
-        quantize(w2q, span(0, P), flat(w2_grouped[0][:]))
         for u in range(2):
             band(bands0[:, 0, span(u, HALF)], h0[u], ALU.add)
             band(bands0[:, 1, span(u, HALF)], h0[u], ALU.subtract)
-            if u == 0:
-                quantize(w2q, span(1, P), flat(w2_grouped[1][:]))
         low1 = keep.tile([P, PAIRS, PACK], BF16, name="low1", align_bytes=64)
         high1 = keep.tile([P, PAIRS, PACK], BF16, name="high1", align_bytes=64)
         low1q, high1q = mx_tiles("low1q", PAIRS), mx_tiles("high1q", PAIRS)
@@ -199,7 +190,7 @@ def tile_picked_haar_gelu_e_kernel(tc, xT, w1, w2, w3, offs, out):
         for s in range(SLICES):
             for a in range(N // P):
                 result = keep.tile([P, PAIRS], F32, name=f"result{s}{a}")
-                if s == SLICES - 1 and a == 1:
+                if s == SLICES - 1 and a == 0:
                     nc.vector.tensor_scalar(result[:], acc[s, a][:], 0.5, None, ALU.mult)
                     nc.sync.dma_start(out[span(a, P), span(s, PAIRS)], result[:])
                 else:

@@ -20,7 +20,7 @@ K_PASS = P * PACK
 PASSES = K // K_PASS
 SLICES = 2
 PAIRS = V // SLICES
-COLS = 2 * PAIRS
+QUARTERS = 4
 HALF = P // 2
 
 
@@ -85,14 +85,14 @@ def tile_picked_haar_gelu_e_kernel(tc, xT, w1, w2, w3, offs, out):
         xq = []
         for g in range(PASSES):
             picked = keep.tile([P, S, PACK], BF16, name=f"picked{g}", align_bytes=64)
-            dst = picked[:].rearrange("p (s d v) t -> p d s v t", s=SLICES, d=2)
+            dst = picked[:].rearrange("p (s d v) t -> p d s v t", s=QUARTERS, d=2)
             for t in range(PACK):
                 nc.vector.tensor_copy(dst[:, :, :, :, t], planes[g, t].indirect(offsets[:]))
             xq.append(mx_tiles(f"xq{g}", S))
             quantize(xq[g], slice(0, S), picked[:].rearrange("p c t -> p (c t)"))
 
         for t in range(2):
-            spare = psum.tile([P, S], F32, name=f"spare{t}", tag=f"bank1{2 + t}")
+            spare = psum.tile([P, S], F32, name=f"spare{t}", tag=f"bank{5 + t}")
             matmul(spare[:], xq[1], slice(0, P), xq[1], slice(0, S), True, True)
 
         def weave_w1(copy, grouped, raw, e):
@@ -121,27 +121,34 @@ def tile_picked_haar_gelu_e_kernel(tc, xT, w1, w2, w3, offs, out):
         for a in range(N // P):
             weave(nc.vector.tensor_copy, w2_grouped[a][:], w2_raw[:, :, span(a, P)])
 
-        banks = {(s, t): psum.tile([P, 2, PAIRS], F32, name=f"bank{s}{t}", tag=f"bank{s}{t}") for s in range(SLICES) for t in range(PACK)}
-        for s in range(SLICES):
-            for g in range(PASSES):
-                for t in range(PACK):
-                    matmul(banks[s, t][:].rearrange("p d v -> p (d v)"), w1q[g][t], slice(0, P), xq[g], span(s, COLS), g == 0, g == PASSES - 1)
+        groups = [(0, 0, 2), (0, 2, 4)] + [(q, 0, PACK) for q in range(1, QUARTERS)]
+        banks = [psum.tile([P, t1 - t0, P], F32, name=f"bank{n}", tag=f"bank{n}") for n, (q, t0, t1) in enumerate(groups)]
+        for g in range(PASSES):
+            for n, (q, t0, t1) in enumerate(groups):
+                for t in range(t0, t1):
+                    matmul(banks[n][:, t - t0], w1q[g][t], slice(0, P), xq[g], span(q, P), (g, t) == (0, t0), (g, t) == (PASSES - 1, t1 - 1))
 
-        def gelu(name, s, v0, v1):
-            h = keep.tile([P, PACK, 2, v1 - v0], F32, name=name)
-            for t in range(PACK):
-                nc.scalar.activation(h[:, t], banks[s, t][:, :, v0:v1], ACT.Gelu_apprx_tanh)
-            return h
+        def gelu(h, n):
+            nc.scalar.activation(h.rearrange("p d v t -> p (d v) t"), banks[n][:].rearrange("p t n -> p n t"), ACT.Gelu_apprx_tanh)
 
-        h0 = [gelu(f"h0{u}", 0, HALF * u, HALF * (u + 1)) for u in range(2)]
-        h1 = gelu("h1", 1, 0, PAIRS)
+        h00 = keep.tile([P, 2, 2, HALF, 2], F32, name="h00")
+        h01 = keep.tile([P, 2, HALF, PACK], F32, name="h01")
+        h1 = keep.tile([P, 2, 2, HALF, PACK], F32, name="h1")
+        for e in range(2):
+            gelu(h00[:, e], e)
+        gelu(h01[:], 2)
+        for u in range(2):
+            gelu(h1[:, u], 3 + u)
+        h0 = [h00[:].rearrange("p e d v t -> p d v e t"), h01[:].rearrange("p d v (e t) -> p d v e t", e=2)]
 
         def flat(grouped):
             return grouped.rearrange("p n j -> p (n j)")
 
         def band(values, h, op):
-            first, second = (h[:, :, d, :].rearrange("p t (c i) -> p c t i", i=2) for d in range(2))
-            nc.vector.tensor_tensor(values.rearrange("p (c i) t -> p c t i", i=2), first, second, op)
+            nc.vector.tensor_tensor(values.rearrange("p v (e t) -> p v e t", e=2), h[:, 0], h[:, 1], op)
+
+        def band_wide(values, op):
+            nc.vector.tensor_tensor(values.rearrange("p (u v) t -> p u v t", u=2), h1[:, :, 0], h1[:, :, 1], op)
 
         w3_grouped = []
         for a in range(N // P):
@@ -162,16 +169,16 @@ def tile_picked_haar_gelu_e_kernel(tc, xT, w1, w2, w3, offs, out):
         high1 = keep.tile([P, PAIRS, PACK], BF16, name="high1", align_bytes=64)
         low1q, high1q = mx_tiles("low1q", PAIRS), mx_tiles("high1q", PAIRS)
         quantize(bands0q, slice(0, 2 * PAIRS), bands0[:].rearrange("p b v t -> p (b v t)"))
-        band(low1[:], h1, ALU.add)
+        band_wide(low1[:], ALU.add)
         quantize(w3q[0], slice(0, P), flat(w3_grouped[0][:]))
-        band(high1[:], h1, ALU.subtract)
+        band_wide(high1[:], ALU.subtract)
         quantize(low1q, slice(0, PAIRS), flat(low1[:]))
         quantize(w3q[1], slice(0, P), flat(w3_grouped[1][:]))
         quantize(high1q, slice(0, PAIRS), flat(high1[:]))
         low = [(bands0q, span(0, PAIRS)), (low1q, span(0, PAIRS))]
         high = [(bands0q, span(1, PAIRS)), (high1q, span(0, PAIRS))]
 
-        acc = {(s, a): psum.tile([P, PAIRS], F32, name=f"acc{s}{a}", tag=f"bank0{2 * s + a}") for s in range(SLICES) for a in range(N // P)}
+        acc = {(s, a): psum.tile([P, PAIRS], F32, name=f"acc{s}{a}", tag=f"bank{(5 + 2 * s + a) % 8}") for s in range(SLICES) for a in range(N // P)}
 
         def low_pass(s, a):
             matmul(acc[s, a][:], w2q, span(a, P), *low[s], True, False)

@@ -22,6 +22,7 @@ SLICES = 2
 PAIRS = V // SLICES
 QUARTERS = 4
 HALF = P // 2
+SPLIT = 96
 
 
 def tile_picked_haar_gelu_e_kernel(tc, xT, w1, w2, w3, offs, out):
@@ -74,9 +75,7 @@ def tile_picked_haar_gelu_e_kernel(tc, xT, w1, w2, w3, offs, out):
                     planes[g, t0 + t] = loaded[:, t]
                 if (g, t0) == (0, 0):
                     nc.sync.dma_start(offsets[:], offs)
-        w1_first = load_w1(0, 0, PACK, 0, P)
-        pieces = ((0, 0, P), (2, 0, 96), (2, 96, P))
-        w1_last = [load_w1(1, j0, j0 + 2, m0, m1) for j0, m0, m1 in pieces]
+        w1_raw = [load_w1(g, 0, PACK, 0, P) for g in range(PASSES)]
         w2_raw = keep.tile([P, PACK, N], F32, name="w2_raw")
         nc.sync.dma_start(w2_raw[:], w2.rearrange("(p j) n -> p j n", j=PACK))
         w3_raw = keep.tile([P, PACK, N], F32, name="w3_raw")
@@ -99,34 +98,34 @@ def tile_picked_haar_gelu_e_kernel(tc, xT, w1, w2, w3, offs, out):
             src = raw.rearrange("p j (m t) -> p m j t", t=PACK)[:, :, :, 2 * e : 2 * e + 2]
             copy(grouped.rearrange("p t m j -> p m j t"), src)
 
-        engines = (nc.vector.tensor_copy, nc.scalar.copy)
-        grouped0 = [keep.tile([P, 2, P, PACK], BF16, name=f"w1_grouped0{e}", align_bytes=64) for e in range(2)]
-        for e in range(2):
-            weave_w1(engines[e], grouped0[e][:], w1_first[:], e)
-        w1q = [[mx_tiles(f"w1q{g}{t}", P) for t in range(PACK)] for g in range(PASSES)]
-        for t in range(PACK):
-            quantize(w1q[0][t], slice(0, P), grouped0[t // 2][:, t % 2].rearrange("p m j -> p (m j)"))
-
-        grouped1 = [keep.tile([P, 2, P, PACK], BF16, name=f"w1_grouped1{e}", tag=f"w1_grouped1{e}", align_bytes=64) for e in range(2)]
-        for raw, (j0, m0, m1) in zip(w1_last, pieces):
+        vec, act = nc.vector.tensor_copy, nc.scalar.copy
+        shares = (
+            ((0, 0, P, vec), (1, 0, P, act)),
+            ((0, 0, P, vec), (1, 0, SPLIT, act), (1, SPLIT, P, vec)),
+        )
+        w1q = []
+        for g in range(PASSES):
+            grouped = [keep.tile([P, 2, P, PACK], BF16, name=f"w1_grouped{g}{e}", align_bytes=64) for e in range(2)]
+            for e, m0, m1, copy in shares[g]:
+                weave_w1(copy, grouped[e][:, :, m0:m1], w1_raw[g][:, :, PACK * m0 : PACK * m1], e)
+            halves = [mx_tiles(f"w1q{g}{e}", 2 * P) for e in range(2)]
             for e in range(2):
-                weave_w1(engines[e], grouped1[e][:, :, m0:m1, j0 : j0 + 2], raw[:], e)
-        for t in range(PACK):
-            quantize(w1q[1][t], slice(0, P), grouped1[t // 2][:, t % 2].rearrange("p m j -> p (m j)"))
+                quantize(halves[e], slice(0, 2 * P), grouped[e][:].rearrange("p t m j -> p (t m j)"))
+            w1q.append([(halves[t // 2], span(t % 2, P)) for t in range(PACK)])
 
         def weave(copy, grouped, raw):
             copy(grouped.rearrange("p (c i) j -> p c j i", i=4), raw.rearrange("p j (c i) -> p c j i", i=4))
 
-        w2_grouped = [keep.tile([P, P, PACK], BF16, name=f"w2_grouped{a}", tag=f"w1_grouped1{a}", align_bytes=64) for a in range(N // P)]
-        for a in range(N // P):
-            weave(nc.vector.tensor_copy, w2_grouped[a][:], w2_raw[:, :, span(a, P)])
+        w2_grouped = keep.tile([P, N, PACK], BF16, name="w2_grouped", align_bytes=64)
+        for a, copy in enumerate((act, vec)):
+            weave(copy, w2_grouped[:, span(a, P)], w2_raw[:, :, span(a, P)])
 
         groups = [(0, 0, 2), (0, 2, 4)] + [(q, 0, PACK) for q in range(1, QUARTERS)]
         banks = [psum.tile([P, t1 - t0, P], F32, name=f"bank{n}", tag=f"bank{n}") for n, (q, t0, t1) in enumerate(groups)]
         for g in range(PASSES):
             for n, (q, t0, t1) in enumerate(groups):
                 for t in range(t0, t1):
-                    matmul(banks[n][:, t - t0], w1q[g][t], slice(0, P), xq[g], span(q, P), (g, t) == (0, t0), (g, t) == (PASSES - 1, t1 - 1))
+                    matmul(banks[n][:, t - t0], *w1q[g][t], xq[g], span(q, P), (g, t) == (0, t0), (g, t) == (PASSES - 1, t1 - 1))
 
         def gelu(h, n):
             nc.scalar.activation(h.rearrange("p d v t -> p (d v) t"), banks[n][:].rearrange("p t n -> p n t"), ACT.Gelu_apprx_tanh)
@@ -150,16 +149,11 @@ def tile_picked_haar_gelu_e_kernel(tc, xT, w1, w2, w3, offs, out):
         def band_wide(values, op):
             nc.vector.tensor_tensor(values.rearrange("p (u v) t -> p u v t", u=2), h1[:, :, 0], h1[:, :, 1], op)
 
-        w3_grouped = []
-        for a in range(N // P):
-            half = keep.tile([P, P, PACK], BF16, name=f"w3_grouped{a}", align_bytes=64)
-            weave(nc.scalar.copy, half[:], w3_raw[:, :, span(a, P)])
-            w3_grouped.append(half)
+        w3_grouped = keep.tile([P, N, PACK], BF16, name="w3_grouped", align_bytes=64)
+        weave(act, w3_grouped[:], w3_raw[:])
 
-        w2q = mx_tiles("w2q", N)
-        for a in range(N // P):
-            quantize(w2q, span(a, P), flat(w2_grouped[a][:]))
-        w3q = [mx_tiles(f"w3q{a}", P) for a in range(N // P)]
+        w2q, w3q = mx_tiles("w2q", N), mx_tiles("w3q", N)
+        quantize(w2q, slice(0, N), flat(w2_grouped[:]))
         bands0 = keep.tile([P, 2, PAIRS, PACK], BF16, name="bands0", align_bytes=64)
         bands0q = mx_tiles("bands0q", 2 * PAIRS)
         for u in range(2):
@@ -170,10 +164,9 @@ def tile_picked_haar_gelu_e_kernel(tc, xT, w1, w2, w3, offs, out):
         low1q, high1q = mx_tiles("low1q", PAIRS), mx_tiles("high1q", PAIRS)
         quantize(bands0q, slice(0, 2 * PAIRS), bands0[:].rearrange("p b v t -> p (b v t)"))
         band_wide(low1[:], ALU.add)
-        quantize(w3q[0], slice(0, P), flat(w3_grouped[0][:]))
         band_wide(high1[:], ALU.subtract)
+        quantize(w3q, slice(0, N), flat(w3_grouped[:]))
         quantize(low1q, slice(0, PAIRS), flat(low1[:]))
-        quantize(w3q[1], slice(0, P), flat(w3_grouped[1][:]))
         quantize(high1q, slice(0, PAIRS), flat(high1[:]))
         low = [(bands0q, span(0, PAIRS)), (low1q, span(0, PAIRS))]
         high = [(bands0q, span(1, PAIRS)), (high1q, span(0, PAIRS))]
@@ -184,16 +177,12 @@ def tile_picked_haar_gelu_e_kernel(tc, xT, w1, w2, w3, offs, out):
             matmul(acc[s, a][:], w2q, span(a, P), *low[s], True, False)
 
         def high_pass(s, a):
-            matmul(acc[s, a][:], w3q[a], slice(0, P), *high[s], False, True)
+            matmul(acc[s, a][:], w3q, span(a, P), *high[s], False, True)
 
-        low_pass(0, 0)
-        low_pass(0, 1)
-        high_pass(0, 0)
-        low_pass(1, 0)
-        low_pass(1, 1)
-        high_pass(0, 1)
-        high_pass(1, 0)
-        high_pass(1, 1)
+        for s in range(SLICES):
+            for one_pass in (low_pass, high_pass):
+                for a in range(N // P):
+                    one_pass(s, a)
         for s in range(SLICES):
             for a in range(N // P):
                 result = keep.tile([P, PAIRS], F32, name=f"result{s}{a}")

@@ -23,6 +23,7 @@ PAIRS = V // SLICES
 QUARTERS = 4
 HALF = P // 2
 SPLIT = 96
+CUT = (PACK - 1) * H + PACK * HALF
 
 
 def tile_picked_haar_gelu_e_kernel(tc, xT, w1, w2, w3, offs, out):
@@ -59,12 +60,7 @@ def tile_picked_haar_gelu_e_kernel(tc, xT, w1, w2, w3, offs, out):
 
         offsets = keep.tile([P, S // 16], U16, name="offsets")
         x_rows = xT.rearrange("(g p t) c -> g p t c", p=P, t=PACK)
-        w1_rows = w1.rearrange("(g p j) c -> g p j c", p=P, j=PACK)
-
-        def load_w1(g, j0, j1, m0, m1):
-            piece = keep.tile([P, j1 - j0, PACK * (m1 - m0)], F32, name=f"w1_piece{g}_{j0}_{m0}")
-            nc.sync.dma_start(piece[:], w1_rows[g, :, j0:j1, PACK * m0 : PACK * m1])
-            return piece
+        w1_rows = w1.rearrange("(g p j) c -> g p (j c)", p=P, j=PACK)
 
         planes = {}
         for g, rows in enumerate((2, 1)):
@@ -75,9 +71,16 @@ def tile_picked_haar_gelu_e_kernel(tc, xT, w1, w2, w3, offs, out):
                     planes[g, t0 + t] = loaded[:, t]
                 if (g, t0) == (0, 0):
                     nc.sync.dma_start(offsets[:], offs)
-        w1_raw = [load_w1(g, 0, PACK, 0, P) for g in range(PASSES)]
-        w2_raw = keep.tile([P, PACK, N], F32, name="w2_raw")
-        nc.sync.dma_start(w2_raw[:], w2.rearrange("(p j) n -> p j n", j=PACK))
+        w1_raw = []
+        for g, cuts in enumerate(((0, PACK * H), (0, CUT, PACK * H))):
+            run = keep.tile([P, PACK * H], F32, name=f"w1_raw{g}")
+            for c0, c1 in zip(cuts, cuts[1:]):
+                nc.sync.dma_start(run[:, c0:c1], w1_rows[g, :, c0:c1])
+            w1_raw.append(run[:].rearrange("p (j c) -> p j c", j=PACK))
+        w2_run = keep.tile([P, PACK * N], F32, name="w2_raw")
+        for c0, c1 in ((0, PACK * N - P), (PACK * N - P, PACK * N)):
+            nc.sync.dma_start(w2_run[:, c0:c1], w2.rearrange("(p j) n -> p (j n)", j=PACK)[:, c0:c1])
+        w2_raw = w2_run[:].rearrange("p (j n) -> p j n", j=PACK)
         w3_raw = keep.tile([P, PACK, N], F32, name="w3_raw")
         nc.sync.dma_start(w3_raw[:], w3.rearrange("(p j) n -> p j n", j=PACK))
 
@@ -101,7 +104,7 @@ def tile_picked_haar_gelu_e_kernel(tc, xT, w1, w2, w3, offs, out):
         vec, act = nc.vector.tensor_copy, nc.scalar.copy
         shares = (
             ((0, 0, P, vec), (1, 0, P, act)),
-            ((0, 0, P, vec), (1, 0, SPLIT, act), (1, SPLIT, P, vec)),
+            ((0, 0, HALF, vec), (1, 0, HALF, act), (0, HALF, P, vec), (1, HALF, SPLIT, act), (1, SPLIT, P, vec)),
         )
         w1q = []
         for g in range(PASSES):
@@ -124,8 +127,9 @@ def tile_picked_haar_gelu_e_kernel(tc, xT, w1, w2, w3, offs, out):
         banks = [psum.tile([P, t1 - t0, P], F32, name=f"bank{n}", tag=f"bank{n}") for n, (q, t0, t1) in enumerate(groups)]
         for g in range(PASSES):
             for n, (q, t0, t1) in enumerate(groups):
-                for t in range(t0, t1):
-                    matmul(banks[n][:, t - t0], *w1q[g][t], xq[g], span(q, P), (g, t) == (0, t0), (g, t) == (PASSES - 1, t1 - 1))
+                order = range(t0, t1) if g == 0 else range(t1 - 1, t0 - 1, -1)
+                for t in order:
+                    matmul(banks[n][:, t - t0], *w1q[g][t], xq[g], span(q, P), (g, t) == (0, t0), (g, t) == (PASSES - 1, t0))
 
         def gelu(h, n):
             nc.scalar.activation(h.rearrange("p d v t -> p (d v) t"), banks[n][:].rearrange("p t n -> p n t"), ACT.Gelu_apprx_tanh)

@@ -94,7 +94,7 @@ def tile_picked_haar_gelu_e_kernel(tc, xT, w1, w2, w3, offs, out):
             quantize(xq[g], slice(0, S), picked[:].rearrange("p c t -> p (c t)"))
 
         for t in range(2):
-            spare = psum.tile([P, S], F32, name=f"spare{t}", tag=f"bank{5 + t}")
+            spare = psum.tile([P, S], F32, name=f"spare{t}", tag=f"bank{QUARTERS + t}")
             matmul(spare[:], xq[1], slice(0, P), xq[1], slice(0, S), True, True)
 
         def weave_w1(copy, grouped, raw, e):
@@ -124,12 +124,16 @@ def tile_picked_haar_gelu_e_kernel(tc, xT, w1, w2, w3, offs, out):
             weave(copy, w2_grouped[:, span(a, P)], w2_raw[:, :, span(a, P)])
 
         groups = [(0, 0, 2), (0, 2, 4)] + [(q, 0, PACK) for q in range(1, QUARTERS)]
-        banks = [psum.tile([P, t1 - t0, P], F32, name=f"bank{n}", tag=f"bank{n}") for n, (q, t0, t1) in enumerate(groups)]
+        banks = [psum.tile([P, t1 - t0, P], F32, name=f"bank{n}", tag=f"bank{n % QUARTERS}") for n, (q, t0, t1) in enumerate(groups)]
+
+        def products(n, g):
+            q, t0, t1 = groups[n]
+            for t in range(t0, t1) if g == 0 else range(t1 - 1, t0 - 1, -1):
+                matmul(banks[n][:, t - t0], *w1q[g][t], xq[g], span(q, P), (g, t) == (0, t0), (g, t) == (PASSES - 1, t0))
+
         for g in range(PASSES):
-            for n, (q, t0, t1) in enumerate(groups):
-                order = range(t0, t1) if g == 0 else range(t1 - 1, t0 - 1, -1)
-                for t in order:
-                    matmul(banks[n][:, t - t0], *w1q[g][t], xq[g], span(q, P), (g, t) == (0, t0), (g, t) == (PASSES - 1, t0))
+            for n in range(QUARTERS):
+                products(n, g)
 
         def gelu(h, n):
             nc.scalar.activation(h.rearrange("p d v t -> p (d v) t"), banks[n][:].rearrange("p t n -> p n t"), ACT.Gelu_apprx_tanh)
@@ -140,6 +144,8 @@ def tile_picked_haar_gelu_e_kernel(tc, xT, w1, w2, w3, offs, out):
         for e in range(2):
             gelu(h00[:, e], e)
         gelu(h01[:], 2)
+        for g in range(PASSES):
+            products(QUARTERS, g)
         for u in range(2):
             gelu(h1[:, u], 3 + u)
         h0 = [h00[:].rearrange("p e d v t -> p d v e t"), h01[:].rearrange("p d v (e t) -> p d v e t", e=2)]
@@ -175,7 +181,7 @@ def tile_picked_haar_gelu_e_kernel(tc, xT, w1, w2, w3, offs, out):
         low = [(bands0q, span(0, PAIRS)), (low1q, span(0, PAIRS))]
         high = [(bands0q, span(1, PAIRS)), (high1q, span(0, PAIRS))]
 
-        acc = {(s, a): psum.tile([P, PAIRS], F32, name=f"acc{s}{a}", tag=f"bank{(5 + 2 * s + a) % 8}") for s in range(SLICES) for a in range(N // P)}
+        acc = {(s, a): psum.tile([P, PAIRS], F32, name=f"acc{s}{a}", tag=f"bank{QUARTERS + 2 * s + a}") for s in range(SLICES) for a in range(N // P)}
 
         def low_pass(s, a):
             matmul(acc[s, a][:], w2q, span(a, P), *low[s], True, False)

@@ -23,6 +23,7 @@ PAIRS = V // SLICES
 QUARTERS = 4
 HALF = P // 2
 SPLIT = 96
+W2_SPLIT = 112
 CUT = (PACK - 1) * H + PACK * HALF
 
 
@@ -78,7 +79,7 @@ def tile_picked_haar_gelu_e_kernel(tc, xT, w1, w2, w3, offs, out):
                 nc.sync.dma_start(run[:, c0:c1], w1_rows[g, :, c0:c1])
             w1_raw.append(run[:].rearrange("p (j c) -> p j c", j=PACK))
         w2_run = keep.tile([P, PACK * N], F32, name="w2_raw")
-        for c0, c1 in ((0, PACK * N - P), (PACK * N - P, PACK * N)):
+        for c0, c1 in ((0, (PACK - 1) * N + W2_SPLIT), ((PACK - 1) * N + W2_SPLIT, PACK * N)):
             nc.sync.dma_start(w2_run[:, c0:c1], w2.rearrange("(p j) n -> p (j n)", j=PACK)[:, c0:c1])
         w2_raw = w2_run[:].rearrange("p (j n) -> p j n", j=PACK)
         w3_raw = keep.tile([P, PACK, N], F32, name="w3_raw")
@@ -120,8 +121,8 @@ def tile_picked_haar_gelu_e_kernel(tc, xT, w1, w2, w3, offs, out):
             copy(grouped.rearrange("p (c i) j -> p c j i", i=4), raw.rearrange("p j (c i) -> p c j i", i=4))
 
         w2_grouped = keep.tile([P, N, PACK], BF16, name="w2_grouped", align_bytes=64)
-        for a, copy in enumerate((act, vec)):
-            weave(copy, w2_grouped[:, span(a, P)], w2_raw[:, :, span(a, P)])
+        for cols, copy in ((slice(0, W2_SPLIT), act), (slice(W2_SPLIT, N), vec)):
+            weave(copy, w2_grouped[:, cols], w2_raw[:, :, cols])
 
         groups = [(0, 0, 2), (0, 2, 4)] + [(q, 0, PACK) for q in range(1, QUARTERS)]
         banks = [psum.tile([P, t1 - t0, P], F32, name=f"bank{n}", tag=f"bank{n % QUARTERS}") for n, (q, t0, t1) in enumerate(groups)]
@@ -160,7 +161,8 @@ def tile_picked_haar_gelu_e_kernel(tc, xT, w1, w2, w3, offs, out):
             nc.vector.tensor_tensor(values.rearrange("p (u v) t -> p u v t", u=2), h1[:, :, 0], h1[:, :, 1], op)
 
         w3_grouped = keep.tile([P, N, PACK], BF16, name="w3_grouped", align_bytes=64)
-        weave(act, w3_grouped[:], w3_raw[:])
+        for a in range(N // P):
+            weave(act, w3_grouped[:, span(a, P)], w3_raw[:, :, span(a, P)])
 
         w2q, w3q = mx_tiles("w2q", N), mx_tiles("w3q", N)
         quantize(w2q, slice(0, N), flat(w2_grouped[:]))
@@ -174,9 +176,10 @@ def tile_picked_haar_gelu_e_kernel(tc, xT, w1, w2, w3, offs, out):
         low1q, high1q = mx_tiles("low1q", PAIRS), mx_tiles("high1q", PAIRS)
         quantize(bands0q, slice(0, 2 * PAIRS), bands0[:].rearrange("p b v t -> p (b v t)"))
         band_wide(low1[:], ALU.add)
+        quantize(w3q, span(0, P), flat(w3_grouped[:, span(0, P)]))
         band_wide(high1[:], ALU.subtract)
-        quantize(w3q, slice(0, N), flat(w3_grouped[:]))
         quantize(low1q, slice(0, PAIRS), flat(low1[:]))
+        quantize(w3q, span(1, P), flat(w3_grouped[:, span(1, P)]))
         quantize(high1q, slice(0, PAIRS), flat(high1[:]))
         low = [(bands0q, span(0, PAIRS)), (low1q, span(0, PAIRS))]
         high = [(bands0q, span(1, PAIRS)), (high1q, span(0, PAIRS))]
@@ -189,10 +192,14 @@ def tile_picked_haar_gelu_e_kernel(tc, xT, w1, w2, w3, offs, out):
         def high_pass(s, a):
             matmul(acc[s, a][:], w3q, span(a, P), *high[s], False, True)
 
-        for s in range(SLICES):
-            for one_pass in (low_pass, high_pass):
-                for a in range(N // P):
-                    one_pass(s, a)
+        low_pass(0, 0)
+        low_pass(0, 1)
+        high_pass(0, 0)
+        low_pass(1, 0)
+        low_pass(1, 1)
+        high_pass(0, 1)
+        high_pass(1, 0)
+        high_pass(1, 1)
         for s in range(SLICES):
             for a in range(N // P):
                 result = keep.tile([P, PAIRS], F32, name=f"result{s}{a}")

@@ -157,9 +157,6 @@ def tile_picked_haar_gelu_e_kernel(tc, xT, w1, w2, w3, offs, out):
         def band(values, h, op):
             nc.vector.tensor_tensor(values.rearrange("p v (e t) -> p v e t", e=2), h[:, 0], h[:, 1], op)
 
-        def band_wide(values, op):
-            nc.vector.tensor_tensor(values.rearrange("p (u v) t -> p u v t", u=2), h1[:, :, 0], h1[:, :, 1], op)
-
         w3_grouped = keep.tile([P, N, PACK], BF16, name="w3_grouped", align_bytes=64)
         for a in range(N // P):
             weave(act, w3_grouped[:, span(a, P)], w3_raw[:, :, span(a, P)])
@@ -174,10 +171,13 @@ def tile_picked_haar_gelu_e_kernel(tc, xT, w1, w2, w3, offs, out):
         low1 = keep.tile([P, PAIRS, PACK], BF16, name="low1", align_bytes=64)
         high1 = keep.tile([P, PAIRS, PACK], BF16, name="high1", align_bytes=64)
         low1q, high1q = mx_tiles("low1q", PAIRS), mx_tiles("high1q", PAIRS)
+        h23 = [h1[:, u].rearrange("p d v (e t) -> p d v e t", e=2) for u in range(2)]
+        band(low1[:, span(0, HALF)], h23[0], ALU.add)
+        band(high1[:, span(0, HALF)], h23[0], ALU.subtract)
         quantize(bands0q, slice(0, 2 * PAIRS), bands0[:].rearrange("p b v t -> p (b v t)"))
-        band_wide(low1[:], ALU.add)
+        band(low1[:, span(1, HALF)], h23[1], ALU.add)
+        band(high1[:, span(1, HALF)], h23[1], ALU.subtract)
         quantize(w3q, span(0, P), flat(w3_grouped[:, span(0, P)]))
-        band_wide(high1[:], ALU.subtract)
         quantize(low1q, slice(0, PAIRS), flat(low1[:]))
         quantize(w3q, span(1, P), flat(w3_grouped[:, span(1, P)]))
         quantize(high1q, slice(0, PAIRS), flat(high1[:]))

@@ -92,11 +92,14 @@ def tile_picked_haar_gelu_e_kernel(tc, xT, w1, w2, w3, offs, out):
             for t in range(PACK):
                 nc.vector.tensor_copy(dst[:, :, :, :, t], planes[g, t].indirect(offsets[:]))
             xq.append(mx_tiles(f"xq{g}", S))
-            quantize(xq[g], slice(0, S), picked[:].rearrange("p c t -> p (c t)"))
+            pieces = 1 if g == 0 else SLICES
+            for u in range(pieces):
+                cols = span(u, S // pieces)
+                quantize(xq[g], cols, picked[:, cols].rearrange("p c t -> p (c t)"))
 
         for t in range(2):
             spare = psum.tile([P, S], F32, name=f"spare{t}", tag=f"bank{QUARTERS + t}")
-            matmul(spare[:], xq[1], slice(0, P), xq[1], slice(0, S), True, True)
+            matmul(spare[:], xq[1], slice(0, P), xq[0], slice(0, S), True, True)
 
         def weave_w1(copy, grouped, raw, e):
             src = raw.rearrange("p j (m t) -> p m j t", t=PACK)[:, :, :, 2 * e : 2 * e + 2]

@@ -128,7 +128,7 @@ def tile_picked_haar_gelu_e_kernel(tc, xT, w1, w2, w3, offs, out):
             weave(copy, w2_grouped[:, cols], w2_raw[:, :, cols])
 
         groups = [(0, 0, 2), (0, 2, 4)] + [(q, 0, PACK) for q in range(1, QUARTERS)]
-        banks = [psum.tile([P, t1 - t0, P], F32, name=f"bank{n}", tag=f"bank{n % QUARTERS}") for n, (q, t0, t1) in enumerate(groups)]
+        banks = [psum.tile([P, t1 - t0, P], F32, name=f"bank{n}", tag=f"bank{n if n < QUARTERS else 1}") for n, (q, t0, t1) in enumerate(groups)]
 
         def products(n, g):
             q, t0, t1 = groups[n]

@@ -117,7 +117,9 @@ def tile_picked_haar_gelu_e_kernel(tc, xT, w1, w2, w3, offs, out):
                 weave_w1(copy, grouped[e][:, :, m0:m1], w1_raw[g][:, :, PACK * m0 : PACK * m1], e)
             halves = [mx_tiles(f"w1q{g}{e}", 2 * P) for e in range(2)]
             for e in range(2):
-                quantize(halves[e], slice(0, 2 * P), grouped[e][:].rearrange("p t m j -> p (t m j)"))
+                last = (g, e) == (PASSES - 1, 1)
+                for cols in (span(0, P), span(1, P)) if last else (slice(0, 2 * P),):
+                    quantize(halves[e], cols, grouped[e][:].rearrange("p t m j -> p (t m) j")[:, cols].rearrange("p c j -> p (c j)"))
             w1q.append([(halves[t // 2], span(t % 2, P)) for t in range(PACK)])
 
         def weave(copy, grouped, raw):
@@ -132,8 +134,9 @@ def tile_picked_haar_gelu_e_kernel(tc, xT, w1, w2, w3, offs, out):
 
         def products(n, g):
             q, t0, t1 = groups[n]
-            for t in range(t0, t1) if g == 0 else range(t1 - 1, t0 - 1, -1):
-                matmul(banks[n][:, t - t0], *w1q[g][t], xq[g], span(q, P), (g, t) == (0, t0), (g, t) == (PASSES - 1, t0))
+            order = range(t0, t1) if g == 0 or q == 0 else range(t1 - 1, t0 - 1, -1)
+            for t in order:
+                matmul(banks[n][:, t - t0], *w1q[g][t], xq[g], span(q, P), (g, t) == (0, t0), (g, t) == (PASSES - 1, order[-1]))
 
         for g in range(PASSES):
             for n in range(QUARTERS):

@@ -97,9 +97,8 @@ def tile_picked_haar_gelu_e_kernel(tc, xT, w1, w2, w3, offs, out):
                 cols = span(u, S // pieces)
                 quantize(xq[g], cols, picked[:, cols].rearrange("p c t -> p (c t)"))
 
-        for t in range(2):
-            spare = psum.tile([P, S], F32, name=f"spare{t}", tag=f"bank{QUARTERS + t}")
-            matmul(spare[:], xq[1], slice(0, P), xq[0], slice(0, S), True, True)
+        spare = psum.tile([P, S], F32, name="spare", tag=f"bank{QUARTERS}")
+        matmul(spare[:], xq[1], slice(0, P), xq[0], slice(0, S), True, True)
 
         def weave_w1(copy, grouped, raw, e):
             src = raw.rearrange("p j (m t) -> p m j t", t=PACK)[:, :, :, 2 * e : 2 * e + 2]

@@ -66,10 +66,10 @@ def tile_picked_haar_gelu_e_kernel(tc, xT, w1, w2, w3, offs, out):
         planes = {}
         for g, rows in enumerate((2, 1)):
             for t0 in range(0, PACK, rows):
-                loaded = keep.tile([P, rows, T], F32, name=f"x{g}{t0}")
-                nc.sync.dma_start(loaded[:], x_rows[g, :, t0 : t0 + rows])
+                loaded = keep.tile([P, rows * T], F32, name=f"x{g}{t0}")
+                nc.sync.dma_start(loaded[:], x_rows[g, :, t0 : t0 + rows].rearrange("p t c -> p (t c)"))
                 for t in range(rows):
-                    planes[g, t0 + t] = loaded[:, t]
+                    planes[g, t0 + t] = loaded[:, span(t, T)]
                 if (g, t0) == (0, 0):
                     nc.sync.dma_start(offsets[:], offs)
         w1_raw = []
@@ -90,7 +90,16 @@ def tile_picked_haar_gelu_e_kernel(tc, xT, w1, w2, w3, offs, out):
             picked = keep.tile([P, S, PACK], BF16, name=f"picked{g}", align_bytes=64)
             dst = picked[:].rearrange("p (s d v) t -> p d s v t", s=QUARTERS, d=2)
             for t in range(PACK):
-                nc.vector.tensor_copy(dst[:, :, :, :, t], planes[g, t].indirect(offsets[:]))
+                if g == 0:
+                    nc.vector.tensor_copy(dst[:, :, :, :, t], planes[g, t].indirect(offsets[:]))
+                else:
+                    plain = keep.tile([P, V], BF16, name=f"plain{t}")
+                    nc.scalar.activation(plain[:], planes[g, t].indirect(offsets[:, span(1, V // 16)]), ACT.Copy)
+                    nc.vector.tensor_copy(dst[:, 0, :, :, t], planes[g, t].indirect(offsets[:, span(0, V // 16)]))
+                    pieces = SLICES if t == PACK - 1 else 1
+                    for u in range(pieces):
+                        moved = plain[:, span(u, V // pieces)].rearrange("p (q v) -> p q v", v=HALF)
+                        nc.vector.tensor_copy(dst[:, 1, span(u, QUARTERS // pieces), :, t], moved)
             xq.append(mx_tiles(f"xq{g}", S))
             pieces = 1 if g == 0 else SLICES
             for u in range(pieces):
@@ -98,7 +107,7 @@ def tile_picked_haar_gelu_e_kernel(tc, xT, w1, w2, w3, offs, out):
                 quantize(xq[g], cols, picked[:, cols].rearrange("p c t -> p (c t)"))
 
         spare = psum.tile([P, S], F32, name="spare", tag=f"bank{QUARTERS}")
-        matmul(spare[:], xq[1], slice(0, P), xq[0], slice(0, S), True, True)
+        matmul(spare[:], xq[1], span(QUARTERS - 1, P), xq[0], slice(0, S), True, True)
 
         def weave_w1(copy, grouped, raw, e):
             src = raw.rearrange("p j (m t) -> p m j t", t=PACK)[:, :, :, 2 * e : 2 * e + 2]

@@ -23,7 +23,8 @@ PAIRS = V // SLICES
 QUARTERS = 4
 HALF = P // 2
 SPLIT = 96
-W2_SPLIT = 112
+FIRST = 80
+W2_SPLIT = 80
 CUT = (PACK - 1) * H + PACK * HALF
 
 
@@ -115,7 +116,7 @@ def tile_picked_haar_gelu_e_kernel(tc, xT, w1, w2, w3, offs, out):
 
         vec, act = nc.vector.tensor_copy, nc.scalar.copy
         shares = (
-            ((0, 0, P, vec), (1, 0, P, act)),
+            ((0, 0, FIRST, vec), (0, FIRST, P, act), (1, 0, HALF, vec), (1, HALF, P, act)),
             ((0, 0, HALF, vec), (1, 0, HALF, act), (0, HALF, P, vec), (1, HALF, SPLIT, act), (1, SPLIT, P, vec)),
         )
         w1q = []
@@ -134,21 +135,24 @@ def tile_picked_haar_gelu_e_kernel(tc, xT, w1, w2, w3, offs, out):
             copy(grouped.rearrange("p (c i) j -> p c j i", i=4), raw.rearrange("p j (c i) -> p c j i", i=4))
 
         w2_grouped = keep.tile([P, N, PACK], BF16, name="w2_grouped", align_bytes=64)
-        for cols, copy in ((slice(0, W2_SPLIT), act), (slice(W2_SPLIT, N), vec)):
+        for cols, copy in ((slice(0, W2_SPLIT), act), (slice(W2_SPLIT, P), vec), (slice(P, N), vec)):
             weave(copy, w2_grouped[:, cols], w2_raw[:, :, cols])
 
         groups = [(0, 0, 2), (0, 2, 4)] + [(q, 0, PACK) for q in range(1, QUARTERS)]
         banks = [psum.tile([P, t1 - t0, P], F32, name=f"bank{n}", tag=f"bank{n if n < QUARTERS else 1}") for n, (q, t0, t1) in enumerate(groups)]
 
-        def products(n, g):
+        def products(n, g, tiles=range(PACK)):
             q, t0, t1 = groups[n]
             order = range(t0, t1) if g == 0 or q == 0 else range(t1 - 1, t0 - 1, -1)
             for t in order:
-                matmul(banks[n][:, t - t0], *w1q[g][t], xq[g], span(q, P), (g, t) == (0, t0), (g, t) == (PASSES - 1, order[-1]))
+                if t in tiles:
+                    matmul(banks[n][:, t - t0], *w1q[g][t], xq[g], span(q, P), (g, t) == (0, t0), (g, t) == (PASSES - 1, order[-1]))
 
-        for g in range(PASSES):
+        for e in range(2):
             for n in range(QUARTERS):
-                products(n, g)
+                products(n, 0, (2 * e, 2 * e + 1))
+        for n in range(QUARTERS):
+            products(n, 1)
 
         def gelu(h, n):
             nc.scalar.activation(h.rearrange("p d v t -> p (d v) t"), banks[n][:].rearrange("p t n -> p n t"), ACT.Gelu_apprx_tanh)
@@ -176,7 +180,8 @@ def tile_picked_haar_gelu_e_kernel(tc, xT, w1, w2, w3, offs, out):
             weave(act, w3_grouped[:, span(a, P)], w3_raw[:, :, span(a, P)])
 
         w2q, w3q = mx_tiles("w2q", N), mx_tiles("w3q", N)
-        quantize(w2q, slice(0, N), flat(w2_grouped[:]))
+        for a in range(N // P):
+            quantize(w2q, span(a, P), flat(w2_grouped[:, span(a, P)]))
         bands0 = keep.tile([P, 2, PAIRS, PACK], BF16, name="bands0", align_bytes=64)
         bands0q = mx_tiles("bands0q", 2 * PAIRS)
         for u in range(2):
@@ -193,8 +198,8 @@ def tile_picked_haar_gelu_e_kernel(tc, xT, w1, w2, w3, offs, out):
         band(high1[:, span(1, HALF)], h23[1], ALU.subtract)
         quantize(w3q, span(0, P), flat(w3_grouped[:, span(0, P)]))
         quantize(low1q, slice(0, PAIRS), flat(low1[:]))
-        quantize(w3q, span(1, P), flat(w3_grouped[:, span(1, P)]))
         quantize(high1q, slice(0, PAIRS), flat(high1[:]))
+        quantize(w3q, span(1, P), flat(w3_grouped[:, span(1, P)]))
         low = [(bands0q, span(0, PAIRS)), (low1q, span(0, PAIRS))]
         high = [(bands0q, span(1, PAIRS)), (high1q, span(0, PAIRS))]
 
@@ -211,15 +216,15 @@ def tile_picked_haar_gelu_e_kernel(tc, xT, w1, w2, w3, offs, out):
         high_pass(0, 0)
         low_pass(1, 0)
         low_pass(1, 1)
-        high_pass(0, 1)
         high_pass(1, 0)
+        high_pass(0, 1)
         high_pass(1, 1)
-        for s in range(SLICES):
-            for a in range(N // P):
+        for a in range(N // P):
+            for s in range(SLICES):
                 result = keep.tile([P, PAIRS], F32, name=f"result{s}{a}")
-                if s == SLICES - 1 and a == 0:
+                if (s, a) == (0, 1):
                     nc.vector.tensor_scalar(result[:], acc[s, a][:], 0.5, None, ALU.mult)
                     nc.sync.dma_start(out[span(a, P), span(s, PAIRS)], result[:])
                 else:
                     nc.scalar.activation(result[:], acc[s, a][:], ACT.Copy, scale=0.5)
-                    (nc.scalar if s == SLICES - 1 else nc.sync).dma_start(out[span(a, P), span(s, PAIRS)], result[:])
+                    (nc.scalar if a == 1 else nc.sync).dma_start(out[span(a, P), span(s, PAIRS)], result[:])

@@ -23,8 +23,7 @@ PAIRS = V // SLICES
 QUARTERS = 4
 HALF = P // 2
 SPLIT = 96
-FIRST = 80
-W2_SPLIT = 80
+W2_SPLIT = 112
 CUT = (PACK - 1) * H + PACK * HALF
 
 
@@ -64,21 +63,25 @@ def tile_picked_haar_gelu_e_kernel(tc, xT, w1, w2, w3, offs, out):
         x_rows = xT.rearrange("(g p t) c -> g p t c", p=P, t=PACK)
         w1_rows = w1.rearrange("(g p j) c -> g p (j c)", p=P, j=PACK)
 
-        planes = {}
+        planes, w1_raw = {}, []
+
+        def load_w1(g, cuts):
+            run = keep.tile([P, PACK * H], F32, name=f"w1_raw{g}")
+            for c0, c1 in zip(cuts, cuts[1:]):
+                nc.sync.dma_start(run[:, c0:c1], w1_rows[g, :, c0:c1])
+            w1_raw.append(run[:].rearrange("p (j c) -> p j c", j=PACK))
+
         for g, rows in enumerate((2, 1)):
             for t0 in range(0, PACK, rows):
+                if (g, t0) == (PASSES - 1, PACK - 1):
+                    load_w1(0, (0, PACK * H))
                 loaded = keep.tile([P, rows * T], F32, name=f"x{g}{t0}")
                 nc.sync.dma_start(loaded[:], x_rows[g, :, t0 : t0 + rows].rearrange("p t c -> p (t c)"))
                 for t in range(rows):
                     planes[g, t0 + t] = loaded[:, span(t, T)]
                 if (g, t0) == (0, 0):
                     nc.sync.dma_start(offsets[:], offs)
-        w1_raw = []
-        for g, cuts in enumerate(((0, PACK * H), (0, CUT, PACK * H))):
-            run = keep.tile([P, PACK * H], F32, name=f"w1_raw{g}")
-            for c0, c1 in zip(cuts, cuts[1:]):
-                nc.sync.dma_start(run[:, c0:c1], w1_rows[g, :, c0:c1])
-            w1_raw.append(run[:].rearrange("p (j c) -> p j c", j=PACK))
+        load_w1(1, (0, CUT, PACK * H))
         w2_run = keep.tile([P, PACK * N], F32, name="w2_raw")
         for c0, c1 in ((0, (PACK - 1) * N + W2_SPLIT), ((PACK - 1) * N + W2_SPLIT, PACK * N)):
             nc.sync.dma_start(w2_run[:, c0:c1], w2.rearrange("(p j) n -> p (j n)", j=PACK)[:, c0:c1])
@@ -107,7 +110,7 @@ def tile_picked_haar_gelu_e_kernel(tc, xT, w1, w2, w3, offs, out):
                 cols = span(u, S // pieces)
                 quantize(xq[g], cols, picked[:, cols].rearrange("p c t -> p (c t)"))
 
-        spare = psum.tile([P, S], F32, name="spare", tag=f"bank{QUARTERS}")
+        spare = psum.tile([P, S], F32, name="spare", tag=f"bank{QUARTERS + 1}")
         matmul(spare[:], xq[1], span(QUARTERS - 1, P), xq[0], slice(0, S), True, True)
 
         def weave_w1(copy, grouped, raw, e):
@@ -116,7 +119,7 @@ def tile_picked_haar_gelu_e_kernel(tc, xT, w1, w2, w3, offs, out):
 
         vec, act = nc.vector.tensor_copy, nc.scalar.copy
         shares = (
-            ((0, 0, FIRST, vec), (0, FIRST, P, act), (1, 0, HALF, vec), (1, HALF, P, act)),
+            ((0, 0, P, act), (1, 0, HALF, vec), (1, HALF, P, act)),
             ((0, 0, HALF, vec), (1, 0, HALF, act), (0, HALF, P, vec), (1, HALF, SPLIT, act), (1, SPLIT, P, vec)),
         )
         w1q = []
@@ -135,11 +138,11 @@ def tile_picked_haar_gelu_e_kernel(tc, xT, w1, w2, w3, offs, out):
             copy(grouped.rearrange("p (c i) j -> p c j i", i=4), raw.rearrange("p j (c i) -> p c j i", i=4))
 
         w2_grouped = keep.tile([P, N, PACK], BF16, name="w2_grouped", align_bytes=64)
-        for cols, copy in ((slice(0, W2_SPLIT), act), (slice(W2_SPLIT, P), vec), (slice(P, N), vec)):
+        for cols, copy in ((slice(0, W2_SPLIT), act), (slice(W2_SPLIT, N), vec)):
             weave(copy, w2_grouped[:, cols], w2_raw[:, :, cols])
 
         groups = [(0, 0, 2), (0, 2, 4)] + [(q, 0, PACK) for q in range(1, QUARTERS)]
-        banks = [psum.tile([P, t1 - t0, P], F32, name=f"bank{n}", tag=f"bank{n if n < QUARTERS else 1}") for n, (q, t0, t1) in enumerate(groups)]
+        banks = [psum.tile([P, t1 - t0, P], F32, name=f"bank{n}", tag=f"bank{n}") for n, (q, t0, t1) in enumerate(groups)]
 
         def products(n, g, tiles=range(PACK)):
             q, t0, t1 = groups[n]
@@ -149,9 +152,9 @@ def tile_picked_haar_gelu_e_kernel(tc, xT, w1, w2, w3, offs, out):
                     matmul(banks[n][:, t - t0], *w1q[g][t], xq[g], span(q, P), (g, t) == (0, t0), (g, t) == (PASSES - 1, order[-1]))
 
         for e in range(2):
-            for n in range(QUARTERS):
+            for n in range(len(groups)):
                 products(n, 0, (2 * e, 2 * e + 1))
-        for n in range(QUARTERS):
+        for n in range(len(groups)):
             products(n, 1)
 
         def gelu(h, n):
@@ -163,8 +166,6 @@ def tile_picked_haar_gelu_e_kernel(tc, xT, w1, w2, w3, offs, out):
         for e in range(2):
             gelu(h00[:, e], e)
         gelu(h01[:], 2)
-        for g in range(PASSES):
-            products(QUARTERS, g)
         for u in range(2):
             gelu(h1[:, u], 3 + u)
         h0 = [h00[:].rearrange("p e d v t -> p d v e t"), h01[:].rearrange("p d v (e t) -> p d v e t", e=2)]
@@ -180,8 +181,7 @@ def tile_picked_haar_gelu_e_kernel(tc, xT, w1, w2, w3, offs, out):
             weave(act, w3_grouped[:, span(a, P)], w3_raw[:, :, span(a, P)])
 
         w2q, w3q = mx_tiles("w2q", N), mx_tiles("w3q", N)
-        for a in range(N // P):
-            quantize(w2q, span(a, P), flat(w2_grouped[:, span(a, P)]))
+        quantize(w2q, slice(0, N), flat(w2_grouped[:]))
         bands0 = keep.tile([P, 2, PAIRS, PACK], BF16, name="bands0", align_bytes=64)
         bands0q = mx_tiles("bands0q", 2 * PAIRS)
         for u in range(2):
@@ -203,7 +203,7 @@ def tile_picked_haar_gelu_e_kernel(tc, xT, w1, w2, w3, offs, out):
         low = [(bands0q, span(0, PAIRS)), (low1q, span(0, PAIRS))]
         high = [(bands0q, span(1, PAIRS)), (high1q, span(0, PAIRS))]
 
-        acc = {(s, a): psum.tile([P, PAIRS], F32, name=f"acc{s}{a}", tag=f"bank{QUARTERS + 2 * s + a}") for s in range(SLICES) for a in range(N // P)}
+        acc = {(s, a): psum.tile([P, PAIRS], F32, name=f"acc{s}{a}", tag=f"bank{(QUARTERS + 1 + 2 * s + a) % 8}") for s in range(SLICES) for a in range(N // P)}
 
         def low_pass(s, a):
             matmul(acc[s, a][:], w2q, span(a, P), *low[s], True, False)

@@ -63,7 +63,7 @@ def tile_picked_haar_gelu_e_kernel(tc, xT, w1, w2, w3, offs, out):
         x_rows = xT.rearrange("(g p t) c -> g p t c", p=P, t=PACK)
         w1_rows = w1.rearrange("(g p j) c -> g p (j c)", p=P, j=PACK)
 
-        planes, w1_raw = {}, []
+        planes, plain_dtype, w1_raw = {}, {}, []
 
         def load_w1(g, cuts):
             run = keep.tile([P, PACK * H], F32, name=f"w1_raw{g}")
@@ -71,14 +71,16 @@ def tile_picked_haar_gelu_e_kernel(tc, xT, w1, w2, w3, offs, out):
                 nc.sync.dma_start(run[:, c0:c1], w1_rows[g, :, c0:c1])
             w1_raw.append(run[:].rearrange("p (j c) -> p j c", j=PACK))
 
-        for g, rows in enumerate((2, 1)):
-            for t0 in range(0, PACK, rows):
+        for g, starts in enumerate(((0, PACK), (0, 2, 3, PACK))):
+            for t0, t1 in zip(starts, starts[1:]):
+                rows = t1 - t0
                 if (g, t0) == (PASSES - 1, PACK - 1):
                     load_w1(0, (0, PACK * H))
                 loaded = keep.tile([P, rows * T], F32, name=f"x{g}{t0}")
                 nc.sync.dma_start(loaded[:], x_rows[g, :, t0 : t0 + rows].rearrange("p t c -> p (t c)"))
                 for t in range(rows):
                     planes[g, t0 + t] = loaded[:, span(t, T)]
+                    plain_dtype[g, t0 + t] = BF16 if rows == 1 else F32
                 if (g, t0) == (0, 0):
                     nc.sync.dma_start(offsets[:], offs)
         load_w1(1, (0, CUT, PACK * H))
@@ -94,16 +96,13 @@ def tile_picked_haar_gelu_e_kernel(tc, xT, w1, w2, w3, offs, out):
             picked = keep.tile([P, S, PACK], BF16, name=f"picked{g}", align_bytes=64)
             dst = picked[:].rearrange("p (s d v) t -> p d s v t", s=QUARTERS, d=2)
             for t in range(PACK):
-                if g == 0:
-                    nc.vector.tensor_copy(dst[:, :, :, :, t], planes[g, t].indirect(offsets[:]))
-                else:
-                    plain = keep.tile([P, V], BF16, name=f"plain{t}")
-                    nc.scalar.activation(plain[:], planes[g, t].indirect(offsets[:, span(1, V // 16)]), ACT.Copy)
-                    nc.vector.tensor_copy(dst[:, 0, :, :, t], planes[g, t].indirect(offsets[:, span(0, V // 16)]))
-                    pieces = SLICES if t == PACK - 1 else 1
-                    for u in range(pieces):
-                        moved = plain[:, span(u, V // pieces)].rearrange("p (q v) -> p q v", v=HALF)
-                        nc.vector.tensor_copy(dst[:, 1, span(u, QUARTERS // pieces), :, t], moved)
+                plain = keep.tile([P, V], plain_dtype[g, t], name=f"plain{g}{t}")
+                nc.scalar.activation(plain[:], planes[g, t].indirect(offsets[:, span(1, V // 16)]), ACT.Copy)
+                nc.vector.tensor_copy(dst[:, 0, :, :, t], planes[g, t].indirect(offsets[:, span(0, V // 16)]))
+                pieces = SLICES if t == PACK - 1 else 1
+                for u in range(pieces):
+                    moved = plain[:, span(u, V // pieces)].rearrange("p (q v) -> p q v", v=HALF)
+                    nc.vector.tensor_copy(dst[:, 1, span(u, QUARTERS // pieces), :, t], moved)
             xq.append(mx_tiles(f"xq{g}", S))
             pieces = 1 if g == 0 else SLICES
             for u in range(pieces):

from contextlib import ExitStack

import concourse.mybir as mybir

K, T, S, V, H, N = 1024, 2048, 512, 256, 512, 256
FLOPS = 2 * K * H * S + 2 * 2 * H * N * V

F32 = mybir.dt.float32
BF16 = mybir.dt.bfloat16
U32 = mybir.dt.uint32
U16 = mybir.dt.uint16
U8 = mybir.dt.uint8
FP8X4 = mybir.dt.float8_e4m3fn_x4
ACT = mybir.ActivationFunctionType
ALU = mybir.AluOpType

P = 128
PACK = 4
K_PASS = P * PACK
PASSES = K // K_PASS
SLICES = 2
PAIRS = V // SLICES
QUARTERS = 4
HALF = P // 2
SPLIT = 96
W2_SPLIT = 112
CUT = (PACK - 1) * H + PACK * HALF


def tile_picked_haar_gelu_e_kernel(tc, xT, w1, w2, w3, offs, out):
    nc = tc.nc
    with ExitStack() as ctx:
        keep = ctx.enter_context(tc.tile_pool(name="keep", bufs=1))
        psum = ctx.enter_context(tc.psum_pool(name="psum", bufs=1))

        def mx_tiles(name, width):
            codes = keep.tile([P, width], U32, name=name + "_codes", align_bytes=64)
            scales = keep.tile([P, width], U8, name=name + "_scales", align_bytes=64)
            return codes, scales

        def quantize(mx, cols, grouped):
            nc.vector.quantize_mx(out=mx[0][:, cols].bitcast(FP8X4), scales=mx[1][:, cols], in_=grouped)

        def matmul(acc, w_mx, w_cols, x_mx, x_cols, start, stop):
            nc.tensor.matmul_mx(
                out=acc,
                lhsT=w_mx[0][:, w_cols].bitcast(FP8X4),
                lhsT_scale=w_mx[1][:, w_cols],
                rhs=x_mx[0][:, x_cols].bitcast(FP8X4),
                rhs_scale=x_mx[1][:, x_cols],
                start=start,
                stop=stop,
            )

        def span(i, width):
            return slice(i * width, (i + 1) * width)

        warm = keep.tile([P, 2], F32, name="warm")
        nc.vector.memset(warm[:, 0:1], 0.0)
        nc.scalar.activation(warm[:, 1:2], warm[:, 0:1], ACT.Gelu_apprx_tanh)

        offsets = keep.tile([P, S // 16], U16, name="offsets")
        x_rows = xT.rearrange("(g p t) c -> g p t c", p=P, t=PACK)
        w1_rows = w1.rearrange("(g p j) c -> g p (j c)", p=P, j=PACK)

        planes, plain_dtype, w1_raw = {}, {}, []

        def load_w1(g, cuts):
            run = keep.tile([P, PACK * H], F32, name=f"w1_raw{g}")
            for c0, c1 in zip(cuts, cuts[1:]):
                nc.sync.dma_start(run[:, c0:c1], w1_rows[g, :, c0:c1])
            w1_raw.append(run[:].rearrange("p (j c) -> p j c", j=PACK))

        for g, starts in enumerate(((0, PACK), (0, 2, 3, PACK))):
            for t0, t1 in zip(starts, starts[1:]):
                rows = t1 - t0
                if (g, t0) == (PASSES - 1, PACK - 1):
                    load_w1(0, (0, PACK * H))
                loaded = keep.tile([P, rows * T], F32, name=f"x{g}{t0}")
                nc.sync.dma_start(loaded[:], x_rows[g, :, t0 : t0 + rows].rearrange("p t c -> p (t c)"))
                for t in range(rows):
                    planes[g, t0 + t] = loaded[:, span(t, T)]
                    plain_dtype[g, t0 + t] = BF16 if rows == 1 else F32
                if (g, t0) == (0, 0):
                    nc.sync.dma_start(offsets[:], offs)
        load_w1(1, (0, CUT, PACK * H))
        w2_run = keep.tile([P, PACK * N], F32, name="w2_raw")
        for c0, c1 in ((0, (PACK - 1) * N + W2_SPLIT), ((PACK - 1) * N + W2_SPLIT, PACK * N)):
            nc.sync.dma_start(w2_run[:, c0:c1], w2.rearrange("(p j) n -> p (j n)", j=PACK)[:, c0:c1])
        w2_raw = w2_run[:].rearrange("p (j n) -> p j n", j=PACK)
        w3_raw = keep.tile([P, PACK, N], F32, name="w3_raw")
        nc.sync.dma_start(w3_raw[:], w3.rearrange("(p j) n -> p j n", j=PACK))

        xq = []
        for g in range(PASSES):
            picked = keep.tile([P, S, PACK], BF16, name=f"picked{g}", align_bytes=64)
            dst = picked[:].rearrange("p (s d v) t -> p d s v t", s=QUARTERS, d=2)
            for t in range(PACK):
                plain = keep.tile([P, V], plain_dtype[g, t], name=f"plain{g}{t}")
                nc.scalar.activation(plain[:], planes[g, t].indirect(offsets[:, span(1, V // 16)]), ACT.Copy)
                nc.vector.tensor_copy(dst[:, 0, :, :, t], planes[g, t].indirect(offsets[:, span(0, V // 16)]))
                pieces = SLICES if t == PACK - 1 else 1
                for u in range(pieces):
                    moved = plain[:, span(u, V // pieces)].rearrange("p (q v) -> p q v", v=HALF)
                    nc.vector.tensor_copy(dst[:, 1, span(u, QUARTERS // pieces), :, t], moved)
            xq.append(mx_tiles(f"xq{g}", S))
            pieces = 1 if g == 0 else SLICES
            for u in range(pieces):
                cols = span(u, S // pieces)
                quantize(xq[g], cols, picked[:, cols].rearrange("p c t -> p (c t)"))

        spare = psum.tile([P, S], F32, name="spare", tag=f"bank{QUARTERS + 1}")
        matmul(spare[:], xq[1], span(QUARTERS - 1, P), xq[0], slice(0, S), True, True)

        def weave_w1(copy, grouped, raw, e):
            src = raw.rearrange("p j (m t) -> p m j t", t=PACK)[:, :, :, 2 * e : 2 * e + 2]
            copy(grouped.rearrange("p t m j -> p m j t"), src)

        vec, act = nc.vector.tensor_copy, nc.scalar.copy
        shares = (
            ((0, 0, P, act), (1, 0, HALF, vec), (1, HALF, P, act)),
            ((0, 0, HALF, vec), (1, 0, HALF, act), (0, HALF, P, vec), (1, HALF, SPLIT, act), (1, SPLIT, P, vec)),
        )
        w1q = []
        for g in range(PASSES):
            grouped = [keep.tile([P, 2, P, PACK], BF16, name=f"w1_grouped{g}{e}", align_bytes=64) for e in range(2)]
            for e, m0, m1, copy in shares[g]:
                weave_w1(copy, grouped[e][:, :, m0:m1], w1_raw[g][:, :, PACK * m0 : PACK * m1], e)
            halves = [mx_tiles(f"w1q{g}{e}", 2 * P) for e in range(2)]
            for e in range(2):
                last = (g, e) == (PASSES - 1, 1)
                for cols in (span(0, P), span(1, P)) if last else (slice(0, 2 * P),):
                    quantize(halves[e], cols, grouped[e][:].rearrange("p t m j -> p (t m) j")[:, cols].rearrange("p c j -> p (c j)"))
            w1q.append([(halves[t // 2], span(t % 2, P)) for t in range(PACK)])

        def weave(copy, grouped, raw):
            copy(grouped.rearrange("p (c i) j -> p c j i", i=4), raw.rearrange("p j (c i) -> p c j i", i=4))

        w2_grouped = keep.tile([P, N, PACK], BF16, name="w2_grouped", align_bytes=64)
        for cols, copy in ((slice(0, W2_SPLIT), act), (slice(W2_SPLIT, N), vec)):
            weave(copy, w2_grouped[:, cols], w2_raw[:, :, cols])

        groups = [(0, 0, 2), (0, 2, 4)] + [(q, 0, PACK) for q in range(1, QUARTERS)]
        banks = [psum.tile([P, t1 - t0, P], F32, name=f"bank{n}", tag=f"bank{n}") for n, (q, t0, t1) in enumerate(groups)]

        def products(n, g, tiles=range(PACK)):
            q, t0, t1 = groups[n]
            order = range(t0, t1) if g == 0 or q == 0 else range(t1 - 1, t0 - 1, -1)
            for t in order:
                if t in tiles:
                    matmul(banks[n][:, t - t0], *w1q[g][t], xq[g], span(q, P), (g, t) == (0, t0), (g, t) == (PASSES - 1, order[-1]))

        for e in range(2):
            for n in range(len(groups)):
                products(n, 0, (2 * e, 2 * e + 1))
        for n in range(len(groups)):
            products(n, 1)

        def gelu(h, n):
            nc.scalar.activation(h.rearrange("p d v t -> p (d v) t"), banks[n][:].rearrange("p t n -> p n t"), ACT.Gelu_apprx_tanh)

        h00 = keep.tile([P, 2, 2, HALF, 2], F32, name="h00")
        h01 = keep.tile([P, 2, HALF, PACK], F32, name="h01")
        h1 = keep.tile([P, 2, 2, HALF, PACK], F32, name="h1")
        for e in range(2):
            gelu(h00[:, e], e)
        gelu(h01[:], 2)
        for u in range(2):
            gelu(h1[:, u], 3 + u)
        h0 = [h00[:].rearrange("p e d v t -> p d v e t"), h01[:].rearrange("p d v (e t) -> p d v e t", e=2)]

        def flat(grouped):
            return grouped.rearrange("p n j -> p (n j)")

        def band(values, h, op):
            nc.vector.tensor_tensor(values.rearrange("p v (e t) -> p v e t", e=2), h[:, 0], h[:, 1], op)

        w3_grouped = keep.tile([P, N, PACK], BF16, name="w3_grouped", align_bytes=64)
        for a in range(N // P):
            weave(act, w3_grouped[:, span(a, P)], w3_raw[:, :, span(a, P)])

        w2q, w3q = mx_tiles("w2q", N), mx_tiles("w3q", N)
        quantize(w2q, slice(0, N), flat(w2_grouped[:]))
        bands0 = keep.tile([P, 2, PAIRS, PACK], BF16, name="bands0", align_bytes=64)
        bands0q = mx_tiles("bands0q", 2 * PAIRS)
        for u in range(2):
            band(bands0[:, 0, span(u, HALF)], h0[u], ALU.add)
            band(bands0[:, 1, span(u, HALF)], h0[u], ALU.subtract)
        low1 = keep.tile([P, PAIRS, PACK], BF16, name="low1", align_bytes=64)
        high1 = keep.tile([P, PAIRS, PACK], BF16, name="high1", align_bytes=64)
        low1q, high1q = mx_tiles("low1q", PAIRS), mx_tiles("high1q", PAIRS)
        h23 = [h1[:, u].rearrange("p d v (e t) -> p d v e t", e=2) for u in range(2)]
        band(low1[:, span(0, HALF)], h23[0], ALU.add)
        band(high1[:, span(0, HALF)], h23[0], ALU.subtract)
        quantize(bands0q, slice(0, 2 * PAIRS), bands0[:].rearrange("p b v t -> p (b v t)"))
        band(low1[:, span(1, HALF)], h23[1], ALU.add)
        band(high1[:, span(1, HALF)], h23[1], ALU.subtract)
        quantize(w3q, span(0, P), flat(w3_grouped[:, span(0, P)]))
        quantize(low1q, slice(0, PAIRS), flat(low1[:]))
        quantize(high1q, slice(0, PAIRS), flat(high1[:]))
        quantize(w3q, span(1, P), flat(w3_grouped[:, span(1, P)]))
        low = [(bands0q, span(0, PAIRS)), (low1q, span(0, PAIRS))]
        high = [(bands0q, span(1, PAIRS)), (high1q, span(0, PAIRS))]

        acc = {(s, a): psum.tile([P, PAIRS], F32, name=f"acc{s}{a}", tag=f"bank{(QUARTERS + 1 + 2 * s + a) % 8}") for s in range(SLICES) for a in range(N // P)}

        def low_pass(s, a):
            matmul(acc[s, a][:], w2q, span(a, P), *low[s], True, False)

        def high_pass(s, a):
            matmul(acc[s, a][:], w3q, span(a, P), *high[s], False, True)

        low_pass(0, 0)
        low_pass(0, 1)
        high_pass(0, 0)
        low_pass(1, 0)
        low_pass(1, 1)
        high_pass(1, 0)
        high_pass(0, 1)
        high_pass(1, 1)
        for a in range(N // P):
            for s in range(SLICES):
                result = keep.tile([P, PAIRS], F32, name=f"result{s}{a}")
                if (s, a) == (0, 1):
                    nc.vector.tensor_scalar(result[:], acc[s, a][:], 0.5, None, ALU.mult)
                    nc.sync.dma_start(out[span(a, P), span(s, PAIRS)], result[:])
                else:
                    nc.scalar.activation(result[:], acc[s, a][:], ACT.Copy, scale=0.5)
                    (nc.scalar if a == 1 else nc.sync).dma_start(out[span(a, P), span(s, PAIRS)], result[:])
